import numpy as np
import ml_dtypes


def mxq(x, axis, fmt="e4m3"):
    dtype, down = {"e4m3": (ml_dtypes.float8_e4m3fn, 7), "e5m2": (ml_dtypes.float8_e5m2, 14)}[fmt]
    v = np.moveaxis(np.asarray(x, np.float32).astype(ml_dtypes.bfloat16).astype(np.float64), axis, -1)
    blocks = v.reshape(v.shape[:-1] + (-1, 32))
    amax = np.abs(blocks).max(-1, keepdims=True)
    byte = np.maximum(np.where(amax > 0, np.frexp(amax)[1] - 1 + 127, 0) - down, 1)
    scale = np.exp2(byte - 127.0)
    codes = (blocks / scale).astype(np.float32).astype(dtype).astype(np.float64)
    return np.moveaxis((codes * scale).reshape(v.shape), -1, axis)


WIDE = False


def mx_kscale(k):
    if not WIDE:
        return np.ones(k)
    levels = np.array([10, -10, 5, -5, 0])
    if k % 512:
        return np.exp2(np.random.permutation(np.resize(levels, k // 32))).repeat(32)
    a = np.empty((k // 512, 16))
    for p in range(k // 512):
        a[p, :8] = np.random.permutation(np.resize(levels, 8))
        for g in range(8):
            far = levels[np.abs(levels - a[p, g]) >= 10]
            a[p, g + 8] = far[np.random.randint(len(far))]
    return np.exp2(a.ravel()).repeat(32)


BF16 = ml_dtypes.bfloat16


def bf(x):
    return np.asarray(x, np.float32).astype(BF16)


def f64(x):
    return np.asarray(x).astype(np.float64)


E2M1 = np.array([0.0, 0.5, 1.0, 1.5, 2.0, 3.0, 4.0, 6.0, -0.0, -0.5, -1.0, -1.5, -2.0, -3.0, -4.0, -6.0])


def pack_weight(w, fmt):
    k, n = w.shape
    w = f64(bf(w)).reshape(k // 32, 32, n)
    amax = np.abs(w).max(1)
    if fmt == "e4m3":
        byte = np.frexp(amax)[1] - 1 + 127 - 7
    else:
        mant, ex = np.frexp(amax / 6.0)
        byte = np.where(mant > 0.5, ex, ex - 1) + 127
    byte = np.clip(np.where(amax > 0, byte, 1), 1, 254)
    scaled = (w * np.exp2(127.0 - byte)[:, None, :]).reshape(k, n).astype(np.float32)
    by_word = np.ascontiguousarray(scaled.reshape(k // 512, 128, 4, n).transpose(0, 1, 3, 2))
    if fmt == "e4m3":
        words = by_word.astype(ml_dtypes.float8_e4m3fn).view(np.uint8)
    else:
        c = by_word.astype(ml_dtypes.float4_e2m1fn).view(np.uint8) & 0xF
        words = c[..., 0::2] | (c[..., 1::2] << 4)
    return np.ascontiguousarray(words), np.ascontiguousarray(byte.astype(np.uint8).reshape(k // 512, 16, n))


def unpack_weight(words, scales, fmt):
    g, p, n, _ = words.shape
    if fmt == "e4m3":
        vals = np.ascontiguousarray(words).view(ml_dtypes.float8_e4m3fn).astype(np.float64)
    else:
        nib = np.empty((g, p, n, 4), np.uint8)
        nib[..., 0::2] = words & 0xF
        nib[..., 1::2] = words >> 4
        vals = E2M1[nib]
    vals = vals * np.repeat(np.exp2(scales.astype(np.float64) - 127.0), 8, axis=1)[..., None]
    return vals.transpose(0, 1, 3, 2).reshape(g * 512, n)
def pack4(w):
    words, scales = pack_weight(w, "e2m1")
    return words.reshape(words.shape[0], 128, -1), scales


def unpack4(words, scales):
    return unpack_weight(words.reshape(words.shape[0], 128, -1, 2), scales, "e2m1")


def planes(Y):
    n, m = Y.shape
    b = f64(bf(Y)).reshape(n // 32, 32, m)
    amax = np.abs(b).max(1)
    byte = np.clip(np.where(amax > 0, np.frexp(amax)[1] - 1 + 127 - 7, 1), 1, 254)
    codes = (b * np.exp2(127.0 - byte)[:, None, :]).reshape(n, m).astype(np.float32).astype(ml_dtypes.float8_e4m3fn).view(np.uint8)
    words = codes.reshape(n // 512, 128, 4, m).transpose(0, 1, 3, 2)
    return np.ascontiguousarray(words), np.ascontiguousarray(byte.astype(np.uint8).reshape(n // 512, 16, m))


W, P, R, M = 2, 512, 512, 1024


def modal_resolvent(alpha, beta, omega):
    s = omega[:, None] - beta[None, :]
    n = np.square(alpha)[None, :] + np.square(s)
    dr = alpha[None, :] / n
    di = -s / n
    return dr, di


def apply_delay(gr, gi, omega, tau):
    phase = omega[:, None] * tau[None, :]
    co = np.cos(phase)[:, None, :]
    si = np.sin(phase)[:, None, :]
    hr = gr * co + gi * si
    hi = gi * co - gr * si
    return hr, hi


def setup_inputs():
    s, t = mx_kscale(R), mx_kscale(M)
    c = bf(np.random.standard_normal((P, R)) * s[None, :])
    b_words, b_scales = pack4(np.random.standard_normal((R, M)) / np.sqrt(R) / s[:, None] * t[None, :])
    k_words, k_scales = pack4(np.random.standard_normal((M, P)) / np.sqrt(M) / t[:, None])
    return {
        "c": c,
        "b_words": b_words,
        "b_scales": b_scales,
        "k_words": k_words,
        "k_scales": k_scales,
        "alpha": bf(np.random.uniform(0.3, 1.0, R)),
        "beta": bf(np.random.uniform(-2.0, 2.0, R)),
        "omega": bf(np.random.uniform(0.5, 2.0, W)),
        "tau": bf(np.random.uniform(0.2, 1.5, M)),
    }


def core(c, b_words, b_scales, k_words, k_scales, alpha, beta, omega, tau):
    c = f64(c)
    alpha, beta, omega, tau = f64(alpha), f64(beta), f64(omega), f64(tau)
    dr, di = modal_resolvent(alpha, beta, omega)
    cr = c[None, :, :] * dr[:, None, :]
    ci = c[None, :, :] * di[:, None, :]
    bq = unpack4(b_words, b_scales)
    gr = mxq(cr, 2, "e4m3") @ bq
    gi = mxq(ci, 2, "e4m3") @ bq
    hr, hi = apply_delay(gr, gi, omega, tau)
    kq = unpack4(k_words, k_scales)
    lr = mxq(hr, 2, "e4m3") @ kq
    li = mxq(hi, 2, "e4m3") @ kq
    delta = np.eye(c.shape[0])[None, :, :]
    return np.sqrt(np.square(delta + lr) + np.square(li) + 1e-6)


def reference(c, b_words, b_scales, k_words, k_scales, alpha, beta, omega, tau):
    R_out = core(c, b_words, b_scales, k_words, k_scales, alpha, beta, omega, tau)
    words, scales = planes(np.moveaxis(R_out, 1, 0).reshape(512, -1))
    return R_out, words, scales

@@ -1,0 +1,623 @@
+import math
+from contextlib import ExitStack
+
+import concourse.mybir as mybir
+from concourse.masks import make_identity
+
+F32 = mybir.dt.float32
+BF16 = mybir.dt.bfloat16
+I32 = mybir.dt.int32
+U32 = mybir.dt.uint32
+U8 = mybir.dt.uint8
+FP8X4 = mybir.dt.float8_e4m3fn_x4
+FP4X4 = mybir.dt.float4_e2m1fn_x4
+ALU = mybir.AluOpType
+ACT = mybir.ActivationFunctionType
+
+W, P, R, M = 2, 512, 512, 1024
+FLOPS = 2 * W * 2 * (P * R * M + P * M * P)
+
+PARTS = 128
+PACK = 4
+GROUPS = M // 512
+HALF = 256
+UNITS = 4
+STEPS = 16
+CRB = [0, 1, 1, 0, 2, 3, 4, 5]
+
+
+def tile_delayedmodalloopreturndifferencemagnitud_x2_kernel(
+    tc, c, b_words, b_scales, k_words, k_scales, alpha, beta, omega, tau, out_0, out_1, out_2
+):
+    nc = tc.nc
+    with ExitStack() as ctx:
+        sb = ctx.enter_context(tc.tile_pool(name="sb", bufs=1))
+        ps = ctx.enter_context(tc.psum_pool(name="ps", bufs=1))
+        ctx.enter_context(tc.manual_schedule())
+
+        def sbuf(name, shape, dtype):
+            return sb.tile(shape, dtype, name=name, align_bytes=64)
+
+        banks = [ps.tile([PARTS, 512], F32, name="bank%d" % i) for i in range(8)]
+        gr_banks, gi_banks = banks[0:2], banks[2:4]
+
+        alpha_sb = sbuf("alpha_sb", [PARTS, PACK], BF16)
+        beta_sb = sbuf("beta_sb", [PARTS, PACK], BF16)
+        omega_sb = sbuf("omega_sb", [PARTS, W], BF16)
+        tau_sb = sbuf("tau_sb", [PARTS, GROUPS, PACK], BF16)
+        c_sb = [sbuf("c_sb%d" % i, [PARTS, 2, R], BF16) for i in range(2)]
+        bw_raw = sbuf("bw_raw", [PARTS, 2 * M], U8)
+        bs_raw = sbuf("bs_raw", [PARTS, M], U8)
+        bw = sbuf("bw", [PARTS, GROUPS, PACK, 256], U8)
+        bs = sbuf("bs", [PARTS, GROUPS, PACK, PARTS], U8)
+        kw = sbuf("kw", [PARTS, GROUPS, 2 * P], U8)
+        ks = sbuf("ks", [PARTS, GROUPS, P], U8)
+        ident = sbuf("ident", [PARTS, PARTS], F32)
+
+        warm = sbuf("warm", [PARTS, 2], F32)
+        warm2 = sbuf("warm2", [PARTS, 1], F32)
+        c_rows = c.rearrange("(q t) r -> q t r", t=PACK)
+
+        def clear_first():
+            nc.vector.memset(bs_raw[:].bitcast(I32), 0)
+            nc.vector.memset(warm[:, 0:1], 1.0)
+            nc.vector.memset(ks[:].rearrange("p g n -> p (g n)").bitcast(I32), 0)
+
+        def load_vectors():
+            nc.scalar.dma_start(out=omega_sb[:], in_=omega.partition_broadcast(PARTS))
+            nc.scalar.dma_start(out=beta_sb[:], in_=beta.rearrange("(p j) -> p j", j=PACK))
+            nc.scalar.dma_start(out=tau_sb[:], in_=tau.rearrange("(g p j) -> p g j", g=GROUPS, j=PACK))
+            nc.scalar.dma_start(out=alpha_sb[:], in_=alpha.rearrange("(p j) -> p j", j=PACK))
+            nc.scalar.activation(out=warm[:, 1:2], in_=warm[:, 0:1], func=ACT.Sin)
+
+        def load_matrices():
+            nc.sync.dma_start(out=c_sb[0][:], in_=c_rows[:, 0:2, :])
+            nc.sync.dma_start(out=bw_raw[:].bitcast(I32), in_=b_words[0].bitcast(I32))
+            nc.sync.dma_start(out=c_sb[1][:], in_=c_rows[:, 2:4, :])
+            for q in range(4):
+                nc.sync.dma_start(
+                    out=bs_raw[32 * q : 32 * q + 4, :].bitcast(I32), in_=b_scales[0, 4 * q : 4 * q + 4, :].bitcast(I32)
+                )
+            nc.sync.dma_start(out=kw[:].bitcast(I32), in_=k_words.rearrange("g p n -> p g n").bitcast(I32))
+            for q in range(4):
+                nc.sync.dma_start(
+                    out=ks[32 * q : 32 * q + 4, :, :].bitcast(I32),
+                    in_=k_scales[:, 4 * q : 4 * q + 4, :].rearrange("g r n -> r g n").bitcast(I32),
+                )
+
+        def identity():
+            make_identity(nc, ident[:])
+
+        def store_scales():
+            for q in range(4):
+                nc.sync.dma_start(
+                    out=out_2[0, 4 * q : 4 * q + 4, :].bitcast(I32),
+                    in_=out_scales[32 * q : 32 * q + 4, :].bitcast(I32),
+                )
+
+        sneg = sbuf("sneg", [PARTS, W, PACK], F32)
+        a2 = sbuf("a2", [PARTS, PACK], F32)
+        s2 = sbuf("s2", [PARTS, W, PACK], F32)
+        den = sbuf("den", [PARTS, W, PACK], F32)
+        rec = sbuf("rec", [PARTS, W, PACK], F32)
+        dfac = [sbuf("dfac%d" % i, [PARTS, W, PACK], F32) for i in range(2)]
+        turns = sbuf("turns", [PARTS, W, 8], F32)
+        whole = sbuf("whole", [PARTS, W, 8], I32)
+        f1 = sbuf("f1", [PARTS, W, 8], F32)
+        f2 = sbuf("f2", [PARTS, W, 8], F32)
+        frac = sbuf("frac", [PARTS, W * 8], F32)
+        fabs = sbuf("fabs", [PARTS, W * 8], F32)
+        co = sbuf("co", [PARTS, W * 8], F32)
+        si = sbuf("si", [PARTS, W * 8], F32)
+        nsi = sbuf("nsi", [PARTS, W * 8], F32)
+
+        def over_w(t):
+            return t[:].unsqueeze(1).to_broadcast([PARTS, W, PACK])
+
+        f1f = f1[:].rearrange("p w j -> p (w j)")
+        f2f = f2[:].rearrange("p w j -> p (w j)")
+
+        def resolvent(step):
+            if step == 0:
+                for w in range(W):
+                    nc.vector.tensor_scalar(
+                        out=sneg[:, w, :],
+                        in0=beta_sb[:],
+                        scalar1=omega_sb[:, w : w + 1],
+                        scalar2=None,
+                        op0=ALU.subtract,
+                    )
+            if step == 1:
+                nc.vector.tensor_tensor(out=s2[:], in0=sneg[:], in1=sneg[:], op=ALU.mult)
+                nc.vector.tensor_tensor(out=a2[:], in0=alpha_sb[:], in1=alpha_sb[:], op=ALU.mult)
+            if step == 2:
+                nc.vector.tensor_tensor(out=den[:], in0=s2[:], in1=over_w(a2), op=ALU.add)
+            if step == 3:
+                nc.vector.reciprocal(out=rec[:], in_=den[:])
+            if step == 4:
+                nc.vector.tensor_tensor(out=dfac[0][:], in0=rec[:], in1=over_w(alpha_sb), op=ALU.mult)
+                nc.vector.tensor_tensor(out=dfac[1][:], in0=rec[:], in1=sneg[:], op=ALU.mult)
+
+        def phase(step):
+            if step == 0:
+                for w in range(W):
+                    nc.vector.tensor_scalar(
+                        out=turns[:, w, :],
+                        in0=tau_sb[:].rearrange("p g j -> p (g j)"),
+                        scalar1=omega_sb[:, w : w + 1],
+                        scalar2=1.0 / (2.0 * math.pi),
+                        op0=ALU.mult,
+                        op1=ALU.mult,
+                    )
+            if step == 1:
+                nc.vector.tensor_copy(out=whole[:], in_=turns[:])
+            if step == 2:
+                nc.vector.tensor_tensor(out=f1[:], in0=turns[:], in1=whole[:], op=ALU.subtract)
+            if step == 3:
+                nc.vector.scalar_tensor_tensor(out=f2f, in0=f1f, scalar=0.5, in1=f1f, op0=ALU.is_gt, op1=ALU.subtract)
+            if step == 4:
+                nc.vector.scalar_tensor_tensor(
+                    out=frac[:], in0=f2f, scalar=0.5, in1=f2f, op0=ALU.is_gt, op1=ALU.subtract
+                )
+            if step == 5:
+                nc.vector.scalar_tensor_tensor(
+                    out=fabs[:], in0=frac[:], scalar=-1.0, in1=frac[:], op0=ALU.mult, op1=ALU.max
+                )
+
+        def sines():
+            nc.scalar.activation(out=si[:], in_=frac[:], func=ACT.Sin, scale=2.0 * math.pi)
+            nc.scalar.activation(out=nsi[:], in_=frac[:], func=ACT.Sin, scale=-2.0 * math.pi)
+            nc.scalar.activation(out=co[:], in_=fabs[:], func=ACT.Sin, scale=-2.0 * math.pi, bias=0.5 * math.pi)
+            nc.scalar.activation(out=warm2[:], in_=warm[:, 0:1], func=ACT.Sqrt)
+
+        def permute_b_words(g):
+            nc.vector.tensor_copy(
+                out=bw[:, g, :, :].rearrange("p t (q e) -> p t q e", e=2),
+                in_=bw_raw[:, 1024 * g : 1024 * (g + 1)].rearrange("p (q t e) -> p t q e", t=PACK, e=2),
+            )
+
+        def permute_b_scales(g):
+            nc.vector.tensor_copy(
+                out=bs[:, g, :, :], in_=bs_raw[:, 512 * g : 512 * (g + 1)].rearrange("p (q t) -> p t q", t=PACK)
+            )
+
+        crb = [sbuf("crb%d" % i, [PARTS, PACK * HALF], BF16) for i in range(2 * UNITS)]
+        crq = [sbuf("crq%d" % i, [PARTS, HALF], U32) for i in range(2 * UNITS)]
+        crs = [sbuf("crs%d" % i, [PARTS, HALF], U8) for i in range(2 * UNITS)]
+
+        crp = [sbuf("crp%d" % i, [PARTS, PACK, HALF], BF16) for i in range(8)]
+
+        def scale_c_planar(u, ri, b):
+            bank = banks[b]
+            for j in range(PACK):
+                nc.scalar.activation(
+                    out=crp[2 * u + ri][:, j, :],
+                    in_=bank[:].bitcast(BF16).rearrange("p (a n e) -> p a e n", a=2, e=2)[:, j // 2, j % 2, :],
+                    func=ACT.Copy,
+                    scale=dfac[ri][:, u // 2, j : j + 1],
+                )
+
+        def interleave_c(u, ri, eng):
+            out = crb[CRB[2 * u + ri]][:].rearrange("p (n t) -> p n t", t=PACK)
+            in_ = crp[2 * u + ri][:].rearrange("p t n -> p n t")
+            if eng == "G":
+                nc.gpsimd.tensor_scalar(out=out, in0=in_, scalar1=1.0, scalar2=0.0, op0=ALU.mult, op1=ALU.add)
+            else:
+                nc.scalar.copy(out=out, in_=in_)
+
+        def transpose_c(u, b):
+            words = c_sb[u % 2][:].bitcast(F32)
+            for tl in range(2):
+                for pair in range(2):
+                    col = 256 * pair + PARTS * tl
+                    nc.tensor.transpose(banks[b][:, col : col + PARTS], words[:, tl, pair::2], ident[:])
+
+        def scale_c(u, ri, b):
+            nc.vector.tensor_tensor(
+                out=crb[CRB[2 * u + ri]][:].rearrange("p (n a e) -> p n a e", a=2, e=2),
+                in0=banks[b][:].bitcast(BF16).rearrange("p (a n e) -> p n a e", a=2, e=2),
+                in1=dfac[ri][:, u // 2, :]
+                .rearrange("p (a e) -> p a e", e=2)
+                .unsqueeze(1)
+                .to_broadcast([PARTS, HALF, 2, 2]),
+                op=ALU.mult,
+            )
+
+        def quantize_c(u, ri):
+            i = 2 * u + ri
+            nc.vector.quantize_mx(out=crq[i][:].bitcast(FP8X4), scales=crs[i][:], in_=crb[CRB[i]][:])
+
+        def fill(h, ri):
+            u, g, j = h // 4, (h // 2) % 2, h % 2
+            bank = (gr_banks, gi_banks)[ri][h % 2]
+            for tl in range(2):
+                t = 2 * j + tl
+                nc.tensor.matmul_mx(
+                    out=bank[:, HALF * tl : HALF * (tl + 1)],
+                    lhsT=bw[:, g, t, :].bitcast(FP4X4),
+                    lhsT_scale=bs[:, g, t, :],
+                    rhs=crq[2 * u + ri][:].bitcast(FP8X4),
+                    rhs_scale=crs[2 * u + ri][:],
+                    start=True,
+                    stop=True,
+                )
+
+        part = [sbuf("part%d" % i, [PARTS, 2, 2, HALF], F32) for i in range(4)]
+        hpl = [sbuf("hpl%d" % i, [PARTS, 2, PACK, HALF], BF16) for i in range(3)]
+        hil = sbuf("hil", [PARTS, 2, HALF, PACK], BF16)
+        hq = [sbuf("hq%d" % i, [PARTS, 2 * HALF], U32) for i in range(2 * UNITS)]
+        hs = [sbuf("hs%d" % i, [PARTS, 2 * HALF], U8) for i in range(2 * UNITS)]
+
+        def factor(tile, h, tl):
+            col = 8 * (h // 8) + PACK * ((h // 2) % 2) + 2 * (h % 2) + tl
+            return tile[:, col : col + 1]
+
+        def scale_gr(h, tls=(0, 1)):
+            for tl in tls:
+                for ri in range(2):
+                    nc.scalar.activation(
+                        out=part[h % 4][:, tl, ri, :],
+                        in_=gr_banks[h % 2][:, HALF * tl : HALF * (tl + 1)],
+                        func=ACT.Copy,
+                        scale=factor((co, nsi)[ri], h, tl),
+                    )
+
+        def scale_gr_vector(h, tl):
+            for ri in range(2):
+                nc.vector.tensor_scalar(
+                    out=part[h % 4][:, tl, ri, :],
+                    in0=gr_banks[h % 2][:, HALF * tl : HALF * (tl + 1)],
+                    scalar1=factor((co, nsi)[ri], h, tl),
+                    scalar2=None,
+                    op0=ALU.mult,
+                )
+
+        def combine(h):
+            for tl in range(2):
+                for ri in range(2):
+                    nc.vector.scalar_tensor_tensor(
+                        out=hpl[(h // 2) % 3][:, ri, 2 * (h % 2) + tl, :],
+                        in0=gi_banks[h % 2][:, HALF * tl : HALF * (tl + 1)],
+                        scalar=factor((si, co)[ri], h, tl),
+                        in1=part[h % 4][:, tl, ri, :],
+                        op0=ALU.mult,
+                        op1=ALU.add,
+                    )
+
+        def interleave_h(s):
+            nc.gpsimd.tensor_scalar(
+                out=hil[:],
+                in0=hpl[s % 3][:].rearrange("p r t n -> p r n t"),
+                scalar1=1.0,
+                scalar2=0.0,
+                op0=ALU.mult,
+                op1=ALU.add,
+            )
+
+        def quantize_h(s):
+            nc.vector.quantize_mx(
+                out=hq[s][:].bitcast(FP8X4), scales=hs[s][:], in_=hil[:].rearrange("p r n t -> p (r n t)")
+            )
+
+        sq = [sbuf("sq%d" % i, [PARTS, 4 * 544], F32) for i in range(2)]
+        diag = [sbuf("diag%d" % i, [PARTS, 4, 2, 32], F32) for i in range(2)]
+        res = [sbuf("res%d" % i, [PARTS, PACK, HALF], F32) for i in range(2 * W)]
+        resb = [sbuf("resb%d" % i, [PARTS, P, PACK], BF16) for i in range(W)]
+        out_codes = sbuf("out_codes", [PARTS, W * P], U32)
+        out_scales = sbuf("out_scales", [PARTS, W * P], U8)
+
+        def loop_gain(u, j, b, groups=(0, 1)):
+            bank = banks[b]
+            for g in groups:
+                nc.tensor.matmul_mx(
+                    out=bank[:],
+                    lhsT=kw[:, g, 256 * j : 256 * (j + 1)].bitcast(FP4X4),
+                    lhsT_scale=ks[:, g, PARTS * j : PARTS * (j + 1)],
+                    rhs=hq[2 * u + g][:].bitcast(FP8X4),
+                    rhs_scale=hs[2 * u + g][:],
+                    start=(g == 0),
+                    stop=(g == GROUPS - 1),
+                )
+
+        def square(u, j, b):
+            bank = banks[b]
+            nc.scalar.activation(out=sq[u % 2][:, 512 * j : 512 * (j + 1)], in_=bank[:], func=ACT.Square)
+
+        def add_identity(u, j, b):
+            bank = banks[b]
+            t0 = 2 * (u % 2)
+            nc.vector.tensor_tensor(
+                out=diag[u % 2][:, j, :, :],
+                in0=bank[:, 0:HALF].rearrange("p (t q) -> p t q", t=2)[:, :, 32 * j : 32 * (j + 1)],
+                in1=ident[:].rearrange("p (q t) -> p t q", t=PACK)[:, t0 : t0 + 2, :],
+                op=ALU.add,
+            )
+
+        def square_diagonal(u, jj):
+            blocks = sq[u % 2][:].rearrange("p (j s) -> p j s", s=544)[:, 2 * jj : 2 * jj + 2, 0:HALF]
+            nc.scalar.activation(
+                out=blocks.rearrange("p j (t q) -> p j t q", t=2)[:, :, :, 0:32],
+                in_=diag[u % 2][:, 2 * jj : 2 * jj + 2, :, :],
+                func=ACT.Square,
+            )
+
+        def sum_squares(u, jj, b):
+            bank = banks[b]
+            for tl in range(2):
+                for jl in range(2):
+                    for ri in range(2):
+                        col = 512 * (2 * jj + jl) + HALF * ri + PARTS * tl
+                        dst = HALF * tl + PARTS * jl
+                        nc.tensor.matmul(
+                            out=bank[:, dst : dst + PARTS],
+                            lhsT=sq[u % 2][:, col : col + PARTS],
+                            rhs=ident[:],
+                            start=(ri == 0),
+                            stop=(ri == 1),
+                            is_transpose=True,
+                        )
+
+        def root(u, jj, b):
+            bank = banks[b]
+            rows = slice(2 * (u % 2), 2 * (u % 2) + 2)
+            nc.scalar.activation(
+                out=res[2 * (u // 2) + jj][:, rows, :],
+                in_=bank[:].rearrange("p (t n) -> p t n", t=2),
+                func=ACT.Sqrt,
+                bias=1e-6,
+            )
+
+        def store_root(u, jj):
+            rows = slice(2 * (u % 2), 2 * (u % 2) + 2)
+            cols = slice(HALF * jj, HALF * (jj + 1))
+            nc.sync.dma_start(
+                out=out_0[u // 2].rearrange("(q t) n -> q t n", t=PACK)[:, rows, cols],
+                in_=res[2 * (u // 2) + jj][:, rows, :],
+            )
+
+        def round_result(w, jj, eng):
+            out = resb[w][:, HALF * jj : HALF * (jj + 1), :]
+            in_ = res[2 * w + jj][:].rearrange("p t n -> p n t")
+            if eng == "G":
+                nc.gpsimd.tensor_scalar(out=out, in0=in_, scalar1=1.0, scalar2=0.0, op0=ALU.mult, op1=ALU.add)
+            else:
+                nc.vector.tensor_copy(out=out, in_=in_)
+
+        def quantize_result(w, lo, hi):
+            cols = slice(P * w + lo, P * w + hi)
+            nc.vector.quantize_mx(
+                out=out_codes[:, cols].bitcast(FP8X4),
+                scales=out_scales[:, cols],
+                in_=resb[w][:, lo:hi, :].rearrange("p n t -> p (n t)"),
+            )
+
+        def store_codes(w, lo, hi):
+            cols = slice(P * w + lo, P * w + hi)
+            nc.sync.dma_start(
+                out=out_1[0].rearrange("p n t -> p (n t)").bitcast(I32)[:, cols], in_=out_codes[:, cols].bitcast(I32)
+            )
+
+        def interleave_h_vector(s):
+            nc.vector.tensor_copy(out=hil[:], in_=hpl[s % 3][:].rearrange("p r t n -> p r n t"))
+
+        clear_first()
+        load_vectors()
+        load_matrices()
+        resolvent(0)
+        resolvent(1)
+        identity()
+        phase(0)
+        transpose_c(0, 4)
+        resolvent(2)
+        phase(1)
+        resolvent(3)
+        transpose_c(1, 5)
+        phase(2)
+        resolvent(4)
+        permute_b_words(0)
+        phase(3)
+        scale_c(0, 0, 4)
+        phase(4)
+        permute_b_scales(0)
+        quantize_c(0, 0)
+        fill(1, 0)
+        fill(0, 0)
+        phase(5)
+        scale_c(0, 1, 4)
+        permute_b_scales(1)
+        scale_c_planar(1, 0, 5)
+        scale_c_planar(1, 1, 5)
+        quantize_c(0, 1)
+        fill(1, 1)
+        interleave_c(1, 0, "G")
+        sines()
+        scale_gr(1, (0, 1))
+        permute_b_words(1)
+        scale_gr(0, (0, 1))
+        fill(0, 1)
+        transpose_c(2, 4)
+        combine(1)
+        fill(3, 0)
+        fill(3, 1)
+        combine(0)
+        scale_gr(3, (0, 1))
+        fill(2, 0)
+        interleave_c(1, 1, "G")
+        scale_gr(2, (0, 1))
+        interleave_h(0)
+        quantize_c(1, 0)
+        combine(3)
+        scale_c_planar(2, 1, 4)
+        fill(2, 1)
+        combine(2)
+        fill(4, 0)
+        quantize_c(1, 1)
+        fill(5, 0)
+        quantize_h(0)
+        interleave_h(1)
+        scale_gr(4, (0, 1))
+        scale_c(2, 0, 4)
+        fill(4, 1)
+        scale_gr(5, (0, 1))
+        fill(5, 1)
+        interleave_c(2, 1, "A")
+        fill(7, 0)
+        combine(4)
+        fill(6, 0)
+        combine(5)
+        quantize_h(1)
+        scale_gr(7, (0, 1))
+        quantize_c(2, 0)
+        transpose_c(3, 4)
+        quantize_c(2, 1)
+        scale_gr(6, (0, 1))
+        fill(7, 1)
+        loop_gain(0, 0, 5, (0, 1))
+        fill(6, 1)
+        combine(7)
+        fill(9, 0)
+        square(0, 0, 5)
+        scale_gr(9, (0, 1))
+        fill(8, 0)
+        fill(9, 1)
+        loop_gain(0, 1, 6, (0, 1))
+        combine(6)
+        square(0, 1, 6)
+        add_identity(0, 0, 5)
+        loop_gain(0, 3, 5, (0, 1))
+        loop_gain(0, 2, 7, (0, 1))
+        interleave_h(2)
+        fill(8, 1)
+        fill(11, 0)
+        scale_c(3, 1, 4)
+        quantize_h(2)
+        add_identity(0, 1, 6)
+        add_identity(0, 3, 5)
+        add_identity(0, 2, 7)
+        scale_gr(8, (0, 1))
+        scale_gr(11, (0,))
+        square_diagonal(0, 0)
+        combine(9)
+        square(0, 2, 7)
+        square(0, 3, 5)
+        interleave_h(3)
+        fill(11, 1)
+        sum_squares(0, 0, 6)
+        scale_c(3, 0, 4)
+        scale_gr_vector(11, 1)
+        combine(8)
+        square_diagonal(0, 1)
+        root(0, 0, 6)
+        store_root(0, 0)
+        fill(10, 0)
+        quantize_h(3)
+        loop_gain(1, 0, 5, (0, 1))
+        fill(10, 1)
+        quantize_c(3, 0)
+        combine(11)
+        scale_gr(10, (0, 1))
+        square(1, 0, 5)
+        fill(13, 0)
+        loop_gain(1, 1, 6, (0, 1))
+        combine(10)
+        add_identity(1, 1, 6)
+        add_identity(1, 0, 5)
+        fill(12, 0)
+        scale_gr(13, (0,))
+        sum_squares(0, 1, 7)
+        quantize_c(3, 1)
+        interleave_h(4)
+        quantize_h(4)
+        square(1, 1, 6)
+        square_diagonal(1, 0)
+        fill(13, 1)
+        root(0, 1, 7)
+        store_root(0, 1)
+        loop_gain(1, 3, 5, (0, 1))
+        fill(12, 1)
+        scale_gr_vector(13, 1)
+        interleave_h(5)
+        scale_gr(12, (0, 1))
+        fill(15, 0)
+        loop_gain(1, 2, 7, (0, 1))
+        square(1, 3, 5)
+        combine(13)
+        combine(12)
+        add_identity(1, 2, 7)
+        quantize_h(5)
+        add_identity(1, 3, 5)
+        scale_gr(15, (0,))
+        fill(14, 0)
+        scale_gr(14, (0, 1))
+        interleave_h(6)
+        fill(14, 1)
+        combine(14)
+        sum_squares(1, 0, 6)
+        loop_gain(2, 0, 5, (0, 1))
+        scale_gr_vector(15, 1)
+        fill(15, 1)
+        square(1, 2, 7)
+        square_diagonal(1, 1)
+        root(1, 0, 6)
+        store_root(1, 0)
+        add_identity(2, 0, 5)
+        square(2, 0, 5)
+        combine(15)
+        quantize_h(6)
+        sum_squares(1, 1, 7)
+        loop_gain(2, 1, 6, (0, 1))
+        loop_gain(2, 3, 5, (0, 1))
+        add_identity(2, 1, 6)
+        loop_gain(3, 3, 2, (0,))
+        loop_gain(3, 1, 0, (0,))
+        square(2, 1, 6)
+        interleave_h_vector(7)
+        quantize_h(7)
+        loop_gain(3, 0, 4, (0,))
+        root(1, 1, 7)
+        store_root(1, 1)
+        loop_gain(3, 2, 1, (0,))
+        square_diagonal(2, 0)
+        loop_gain(2, 2, 7, (0, 1))
+        loop_gain(3, 0, 4, (1,))
+        loop_gain(3, 1, 0, (1,))
+        loop_gain(3, 3, 2, (1,))
+        loop_gain(3, 2, 1, (1,))
+        square(2, 3, 5)
+        square(2, 2, 7)
+        round_result(0, 1, "G")
+        add_identity(2, 3, 5)
+        add_identity(3, 1, 0)
+        add_identity(2, 2, 7)
+        square(3, 0, 4)
+        sum_squares(2, 0, 6)
+        square(3, 1, 0)
+        add_identity(3, 2, 1)
+        add_identity(3, 0, 4)
+        square_diagonal(2, 1)
+        round_result(0, 0, "G")
+        square_diagonal(3, 0)
+        add_identity(3, 3, 2)
+        sum_squares(3, 0, 5)
+        quantize_result(0, 0, 512)
+        store_codes(0, 0, 512)
+        square(3, 2, 1)
+        square(3, 3, 2)
+        sum_squares(2, 1, 7)
+        square_diagonal(3, 1)
+        sum_squares(3, 1, 3)
+        root(2, 0, 6)
+        store_root(2, 0)
+        root(3, 0, 5)
+        store_root(3, 0)
+        root(2, 1, 7)
+        store_root(2, 1)
+        round_result(1, 0, "V")
+        quantize_result(1, 0, 256)
+        store_codes(1, 0, 256)
+        root(3, 1, 3)
+        store_root(3, 1)
+        round_result(1, 1, "V")
+        quantize_result(1, 256, 512)
+        store_codes(1, 256, 512)
+        store_scales()

@@ -23,7 +23,8 @@ GROUPS = M // 512
 HALF = 256
 UNITS = 4
 STEPS = 16
-CRB = [0, 1, 1, 0, 2, 3, 4, 5]
+CRB = [0,1,2,3,1,0,4,5]
+CHUNKS = [[[0,2],[2,2]],[[0,2],[2,1],[3,1]]]
 
 
 def tile_delayedmodalloopreturndifferencemagnitud_x2_kernel(
@@ -43,7 +44,9 @@ def tile_delayedmodalloopreturndifferencemagnitud_x2_kernel(
 
         alpha_sb = sbuf("alpha_sb", [PARTS, PACK], BF16)
         beta_sb = sbuf("beta_sb", [PARTS, PACK], BF16)
-        omega_sb = sbuf("omega_sb", [PARTS, W], BF16)
+        omega_word = sbuf("omega_word", [PARTS, 1], F32)
+        omega_sb = sbuf("omega_sb", [PARTS, W], F32)
+        omega_neg = sbuf("omega_neg", [PARTS, W], F32)
         tau_sb = sbuf("tau_sb", [PARTS, GROUPS, PACK], BF16)
         c_sb = [sbuf("c_sb%d" % i, [PARTS, 2, R], BF16) for i in range(2)]
         bw_raw = sbuf("bw_raw", [PARTS, 2 * M], U8)
@@ -54,30 +57,33 @@ def tile_delayedmodalloopreturndifferencemagnitud_x2_kernel(
         ks = sbuf("ks", [PARTS, GROUPS, P], U8)
         ident = sbuf("ident", [PARTS, PARTS], F32)
 
+        ident2 = sbuf("ident2", [PARTS, PARTS], F32)
+        cross = sbuf("cross", [PARTS, 4, 2, PARTS], F32)
         warm = sbuf("warm", [PARTS, 2], F32)
         warm2 = sbuf("warm2", [PARTS, 1], F32)
         c_rows = c.rearrange("(q t) r -> q t r", t=PACK)
 
         def clear_first():
+            nc.vector.memset(omega_word[:], 0.0)
             nc.vector.memset(bs_raw[:].bitcast(I32), 0)
             nc.vector.memset(warm[:, 0:1], 1.0)
             nc.vector.memset(ks[:].rearrange("p g n -> p (g n)").bitcast(I32), 0)
 
         def load_vectors():
-            nc.scalar.dma_start(out=omega_sb[:], in_=omega.partition_broadcast(PARTS))
             nc.scalar.dma_start(out=beta_sb[:], in_=beta.rearrange("(p j) -> p j", j=PACK))
-            nc.scalar.dma_start(out=tau_sb[:], in_=tau.rearrange("(g p j) -> p g j", g=GROUPS, j=PACK))
             nc.scalar.dma_start(out=alpha_sb[:], in_=alpha.rearrange("(p j) -> p j", j=PACK))
+            nc.scalar.dma_start(out=omega_word[0:1, :].bitcast(BF16), in_=omega.rearrange("(o w) -> o w", o=1))
             nc.scalar.activation(out=warm[:, 1:2], in_=warm[:, 0:1], func=ACT.Sin)
 
         def load_matrices():
             nc.sync.dma_start(out=c_sb[0][:], in_=c_rows[:, 0:2, :])
             nc.sync.dma_start(out=bw_raw[:].bitcast(I32), in_=b_words[0].bitcast(I32))
-            nc.sync.dma_start(out=c_sb[1][:], in_=c_rows[:, 2:4, :])
             for q in range(4):
                 nc.sync.dma_start(
                     out=bs_raw[32 * q : 32 * q + 4, :].bitcast(I32), in_=b_scales[0, 4 * q : 4 * q + 4, :].bitcast(I32)
                 )
+            nc.sync.dma_start(out=tau_sb[:], in_=tau.rearrange("(g p j) -> p g j", g=GROUPS, j=PACK))
+            nc.sync.dma_start(out=c_sb[1][:], in_=c_rows[:, 2:4, :])
             nc.sync.dma_start(out=kw[:].bitcast(I32), in_=k_words.rearrange("g p n -> p g n").bitcast(I32))
             for q in range(4):
                 nc.sync.dma_start(
@@ -85,8 +91,20 @@ def tile_delayedmodalloopreturndifferencemagnitud_x2_kernel(
                     in_=k_scales[:, 4 * q : 4 * q + 4, :].rearrange("g r n -> r g n").bitcast(I32),
                 )
 
+        def spread_omega(b):
+            nc.tensor.transpose(banks[b][:, 0:PARTS], omega_word[:, 0:1].to_broadcast([PARTS, PARTS]), ident[:])
+
+        def copy_omega(b):
+            omega_all = banks[b][:, 0:1].bitcast(BF16)
+            nc.scalar.activation(out=omega_neg[:], in_=omega_all, func=ACT.Copy, scale=-1.0)
+            nc.scalar.activation(out=omega_sb[:], in_=omega_all, func=ACT.Copy)
+
         def identity():
             make_identity(nc, ident[:])
+
+        def clear_cross():
+            nc.gpsimd.memset(cross[:], 0.0)
+            nc.gpsimd.tensor_scalar(out=ident2[:], in0=ident[:], scalar1=2.0, scalar2=0.0, op0=ALU.mult, op1=ALU.add)
 
         def store_scales():
             for q in range(4):
@@ -119,17 +137,14 @@ def tile_delayedmodalloopreturndifferencemagnitud_x2_kernel(
 
         def resolvent(step):
             if step == 0:
-                for w in range(W):
-                    nc.vector.tensor_scalar(
-                        out=sneg[:, w, :],
-                        in0=beta_sb[:],
-                        scalar1=omega_sb[:, w : w + 1],
-                        scalar2=None,
-                        op0=ALU.subtract,
-                    )
+                nc.scalar.activation(out=a2[:], in_=alpha_sb[:], func=ACT.Square)
             if step == 1:
-                nc.vector.tensor_tensor(out=s2[:], in0=sneg[:], in1=sneg[:], op=ALU.mult)
-                nc.vector.tensor_tensor(out=a2[:], in0=alpha_sb[:], in1=alpha_sb[:], op=ALU.mult)
+                for w in range(W):
+                    nc.scalar.activation(out=s2[:, w, :], in_=beta_sb[:], func=ACT.Square, bias=omega_neg[:, w : w + 1])
+                for w in range(W):
+                    nc.scalar.activation(
+                        out=sneg[:, w, :], in_=beta_sb[:], func=ACT.Identity, bias=omega_neg[:, w : w + 1]
+                    )
             if step == 2:
                 nc.vector.tensor_tensor(out=den[:], in0=s2[:], in1=over_w(a2), op=ALU.add)
             if step == 3:
@@ -160,9 +175,7 @@ def tile_delayedmodalloopreturndifferencemagnitud_x2_kernel(
                     out=frac[:], in0=f2f, scalar=0.5, in1=f2f, op0=ALU.is_gt, op1=ALU.subtract
                 )
             if step == 5:
-                nc.vector.scalar_tensor_tensor(
-                    out=fabs[:], in0=frac[:], scalar=-1.0, in1=frac[:], op0=ALU.mult, op1=ALU.max
-                )
+                nc.scalar.activation(out=fabs[:], in_=frac[:], func=ACT.Abs)
 
         def sines():
             nc.scalar.activation(out=si[:], in_=frac[:], func=ACT.Sin, scale=2.0 * math.pi)
@@ -272,8 +285,8 @@ def tile_delayedmodalloopreturndifferencemagnitud_x2_kernel(
                     op0=ALU.mult,
                 )
 
-        def combine(h):
-            for tl in range(2):
+        def combine(h, tls):
+            for tl in tls:
                 for ri in range(2):
                     nc.vector.scalar_tensor_tensor(
                         out=hpl[(h // 2) % 3][:, ri, 2 * (h % 2) + tl, :],
@@ -299,9 +312,12 @@ def tile_delayedmodalloopreturndifferencemagnitud_x2_kernel(
                 out=hq[s][:].bitcast(FP8X4), scales=hs[s][:], in_=hil[:].rearrange("p r n t -> p (r n t)")
             )
 
-        sq = [sbuf("sq%d" % i, [PARTS, 4 * 544], F32) for i in range(2)]
-        diag = [sbuf("diag%d" % i, [PARTS, 4, 2, 32], F32) for i in range(2)]
-        res = [sbuf("res%d" % i, [PARTS, PACK, HALF], F32) for i in range(2 * W)]
+        sq = [sbuf("sq%d" % i, [PARTS, 4 * 512], F32) for i in range(2)]
+        res = {
+            (w, j0): sbuf("res%d_%d" % (w, j0), [PARTS, PACK, PARTS * nj], F32)
+            for w in range(W)
+            for j0, nj in CHUNKS[w]
+        }
         resb = [sbuf("resb%d" % i, [PARTS, P, PACK], BF16) for i in range(W)]
         out_codes = sbuf("out_codes", [PARTS, W * P], U32)
         out_scales = sbuf("out_scales", [PARTS, W * P], U8)
@@ -323,301 +339,375 @@ def tile_delayedmodalloopreturndifferencemagnitud_x2_kernel(
             bank = banks[b]
             nc.scalar.activation(out=sq[u % 2][:, 512 * j : 512 * (j + 1)], in_=bank[:], func=ACT.Square)
 
-        def add_identity(u, j, b):
-            bank = banks[b]
-            t0 = 2 * (u % 2)
+        raw = [sbuf("raw%d" % i, [PARTS, 512], F32) for i in range(4)]
+
+        def copy_gain(u, j, b):
+            nc.vector.tensor_copy(out=raw[j][:], in_=banks[b][:])
+
+        def square_vector(u, j):
             nc.vector.tensor_tensor(
-                out=diag[u % 2][:, j, :, :],
-                in0=bank[:, 0:HALF].rearrange("p (t q) -> p t q", t=2)[:, :, 32 * j : 32 * (j + 1)],
-                in1=ident[:].rearrange("p (q t) -> p t q", t=PACK)[:, t0 : t0 + 2, :],
-                op=ALU.add,
+                out=sq[u % 2][:, 512 * j : 512 * (j + 1)], in0=raw[j][:], in1=raw[j][:], op=ALU.mult
             )
 
-        def square_diagonal(u, jj):
-            blocks = sq[u % 2][:].rearrange("p (j s) -> p j s", s=544)[:, 2 * jj : 2 * jj + 2, 0:HALF]
-            nc.scalar.activation(
-                out=blocks.rearrange("p j (t q) -> p j t q", t=2)[:, :, :, 0:32],
-                in_=diag[u % 2][:, 2 * jj : 2 * jj + 2, :, :],
-                func=ACT.Square,
+        def add_identity(u, j, b):
+            t0 = 2 * (u % 2)
+            nc.vector.scalar_tensor_tensor(
+                out=cross[:, j, :, 32 * j : 32 * (j + 1)],
+                in0=banks[b][:, 0:HALF].rearrange("p (t q) -> p t q", t=2)[:, :, 32 * j : 32 * (j + 1)],
+                scalar=0.5,
+                in1=ident2[:].rearrange("p (q t) -> p t q", t=PACK)[:, t0 : t0 + 2, :],
+                op0=ALU.add,
+                op1=ALU.mult,
             )
 
-        def sum_squares(u, jj, b):
-            bank = banks[b]
+        def sum_squares(u, j0, nj, b):
             for tl in range(2):
-                for jl in range(2):
-                    for ri in range(2):
-                        col = 512 * (2 * jj + jl) + HALF * ri + PARTS * tl
-                        dst = HALF * tl + PARTS * jl
+                for jl in range(nj):
+                    j = j0 + jl
+                    col = 512 * j + PARTS * tl
+                    terms = (
+                        sq[u % 2][:, col : col + PARTS],
+                        sq[u % 2][:, col + HALF : col + HALF + PARTS],
+                        cross[:, j, tl, :],
+                    )
+                    dst = PARTS * (nj * tl + jl)
+                    for i, term in enumerate(terms):
                         nc.tensor.matmul(
-                            out=bank[:, dst : dst + PARTS],
-                            lhsT=sq[u % 2][:, col : col + PARTS],
+                            out=banks[b][:, dst : dst + PARTS],
+                            lhsT=term,
                             rhs=ident[:],
-                            start=(ri == 0),
-                            stop=(ri == 1),
+                            start=(i == 0),
+                            stop=(i == 2),
                             is_transpose=True,
                         )
 
-        def root(u, jj, b):
-            bank = banks[b]
+        def root(u, j0, nj, b):
             rows = slice(2 * (u % 2), 2 * (u % 2) + 2)
             nc.scalar.activation(
-                out=res[2 * (u // 2) + jj][:, rows, :],
-                in_=bank[:].rearrange("p (t n) -> p t n", t=2),
+                out=res[u // 2, j0][:, rows, :],
+                in_=banks[b][:, 0 : HALF * nj].rearrange("p (t n) -> p t n", t=2),
                 func=ACT.Sqrt,
                 bias=1e-6,
             )
 
-        def store_root(u, jj):
+        def store_root(u, j0, nj):
             rows = slice(2 * (u % 2), 2 * (u % 2) + 2)
-            cols = slice(HALF * jj, HALF * (jj + 1))
+            cols = slice(PARTS * j0, PARTS * (j0 + nj))
             nc.sync.dma_start(
                 out=out_0[u // 2].rearrange("(q t) n -> q t n", t=PACK)[:, rows, cols],
-                in_=res[2 * (u // 2) + jj][:, rows, :],
+                in_=res[u // 2, j0][:, rows, :],
             )
 
-        def round_result(w, jj, eng):
-            out = resb[w][:, HALF * jj : HALF * (jj + 1), :]
-            in_ = res[2 * w + jj][:].rearrange("p t n -> p n t")
+        def round_result(w, j0, nj, eng):
+            out = resb[w][:, PARTS * j0 : PARTS * (j0 + nj), :]
+            in_ = res[w, j0][:].rearrange("p t n -> p n t")
             if eng == "G":
                 nc.gpsimd.tensor_scalar(out=out, in0=in_, scalar1=1.0, scalar2=0.0, op0=ALU.mult, op1=ALU.add)
+            elif eng == "A":
+                nc.scalar.copy(out=out, in_=in_)
             else:
                 nc.vector.tensor_copy(out=out, in_=in_)
 
-        def quantize_result(w, lo, hi):
-            cols = slice(P * w + lo, P * w + hi)
+        def quantize_result(w, j0, nj):
+            cols = slice(P * w + PARTS * j0, P * w + PARTS * (j0 + nj))
             nc.vector.quantize_mx(
                 out=out_codes[:, cols].bitcast(FP8X4),
                 scales=out_scales[:, cols],
-                in_=resb[w][:, lo:hi, :].rearrange("p n t -> p (n t)"),
+                in_=resb[w][:, PARTS * j0 : PARTS * (j0 + nj), :].rearrange("p n t -> p (n t)"),
             )
 
-        def store_codes(w, lo, hi):
-            cols = slice(P * w + lo, P * w + hi)
+        def store_codes(w, j0, nj):
+            cols = slice(P * w + PARTS * j0, P * w + PARTS * (j0 + nj))
             nc.sync.dma_start(
                 out=out_1[0].rearrange("p n t -> p (n t)").bitcast(I32)[:, cols], in_=out_codes[:, cols].bitcast(I32)
+            )
+
+        ct_sb = [sbuf("ct_sb%d" % i, [PARTS, HALF, PACK], BF16) for i in range(2)]
+
+        def copy_ct(half, b):
+            nc.scalar.copy(out=ct_sb[half][:].bitcast(F32), in_=banks[b][:].rearrange("p (a n) -> p n a", a=2))
+
+        def scale_c_gpsimd(u, ri):
+            nc.gpsimd.tensor_tensor(
+                out=crb[CRB[2 * u + ri]][:].rearrange("p (n t) -> p n t", t=PACK),
+                in0=ct_sb[u % 2][:],
+                in1=dfac[ri][:, u // 2, :].unsqueeze(1).to_broadcast([PARTS, HALF, PACK]),
+                op=ALU.mult,
+            )
+
+        def interleave_h_part(s, ri, eng):
+            out = hil[:, ri, :, :]
+            in_ = hpl[s % 3][:, ri, :, :].rearrange("p t n -> p n t")
+            if eng == "A":
+                nc.scalar.copy(out=out, in_=in_)
+            else:
+                nc.vector.tensor_copy(out=out, in_=in_)
+
+        def quantize_h_part(s, ri):
+            cols = slice(HALF * ri, HALF * (ri + 1))
+            nc.vector.quantize_mx(
+                out=hq[s][:, cols].bitcast(FP8X4),
+                scales=hs[s][:, cols],
+                in_=hil[:, ri, :, :].rearrange("p n t -> p (n t)"),
             )
 
         def interleave_h_vector(s):
             nc.vector.tensor_copy(out=hil[:], in_=hpl[s % 3][:].rearrange("p r t n -> p r n t"))
 
         clear_first()
-        load_vectors()
         load_matrices()
-        resolvent(0)
-        resolvent(1)
         identity()
+        load_vectors()
+        spread_omega(6)
+        resolvent(0)
+        permute_b_words(0)
+        copy_omega(6)
         phase(0)
+        resolvent(1)
         transpose_c(0, 4)
         resolvent(2)
         phase(1)
         resolvent(3)
-        transpose_c(1, 5)
         phase(2)
         resolvent(4)
-        permute_b_words(0)
         phase(3)
-        scale_c(0, 0, 4)
-        phase(4)
-        permute_b_scales(0)
-        quantize_c(0, 0)
-        fill(1, 0)
-        fill(0, 0)
-        phase(5)
-        scale_c(0, 1, 4)
         permute_b_scales(1)
-        scale_c_planar(1, 0, 5)
-        scale_c_planar(1, 1, 5)
+        phase(4)
+        transpose_c(0, 5)
+        scale_c(0, 0, 4)
+        scale_c(0, 1, 4)
+        transpose_c(1, 4)
+        clear_cross()
+        quantize_c(0, 0)
+        permute_b_scales(0)
         quantize_c(0, 1)
-        fill(1, 1)
-        interleave_c(1, 0, "G")
-        sines()
-        scale_gr(1, (0, 1))
+        scale_c_planar(2, 0, 5)
+        phase(5)
         permute_b_words(1)
-        scale_gr(0, (0, 1))
+        fill(0, 0)
+        scale_c_planar(2, 1, 5)
         fill(0, 1)
-        transpose_c(2, 4)
-        combine(1)
-        fill(3, 0)
-        fill(3, 1)
-        combine(0)
-        scale_gr(3, (0, 1))
+        sines()
+        scale_c(1, 0, 4)
+        fill(1, 0)
+        scale_gr(0, (1,))
+        scale_gr(0, (0,))
+        fill(1, 1)
+        scale_gr(1, (1,))
+        combine(0, (1,))
+        interleave_c(2, 0, "G")
+        combine(0, (0,))
+        scale_gr(1, (0,))
+        combine(1, (1,))
         fill(2, 0)
-        interleave_c(1, 1, "G")
-        scale_gr(2, (0, 1))
-        interleave_h(0)
+        combine(1, (0,))
+        fill(3, 0)
         quantize_c(1, 0)
-        combine(3)
-        scale_c_planar(2, 1, 4)
         fill(2, 1)
-        combine(2)
+        interleave_c(2, 1, "G")
+        scale_c(1, 1, 4)
+        scale_gr(2, (1,))
+        scale_gr(2, (0,))
+        fill(3, 1)
         fill(4, 0)
-        quantize_c(1, 1)
+        combine(2, (1,))
+        scale_gr(3, (1,))
+        scale_gr(3, (0,))
+        interleave_h(0)
         fill(5, 0)
-        quantize_h(0)
-        interleave_h(1)
-        scale_gr(4, (0, 1))
-        scale_c(2, 0, 4)
-        fill(4, 1)
-        scale_gr(5, (0, 1))
-        fill(5, 1)
-        interleave_c(2, 1, "A")
-        fill(7, 0)
-        combine(4)
+        scale_gr(4, (0,))
+        scale_gr(4, (1,))
+        combine(2, (0,))
         fill(6, 0)
-        combine(5)
-        quantize_h(1)
-        scale_gr(7, (0, 1))
+        combine(3, (0,))
+        combine(3, (1,))
+        scale_gr(5, (0,))
+        quantize_c(1, 1)
+        scale_gr(5, (1,))
+        scale_gr(6, (0,))
+        quantize_h(0)
+        fill(4, 1)
         quantize_c(2, 0)
-        transpose_c(3, 4)
-        quantize_c(2, 1)
-        scale_gr(6, (0, 1))
-        fill(7, 1)
-        loop_gain(0, 0, 5, (0, 1))
-        fill(6, 1)
-        combine(7)
+        scale_gr(6, (1,))
+        fill(7, 0)
+        fill(5, 1)
+        scale_gr(7, (1,))
+        scale_gr(7, (0,))
+        scale_c(3, 1, 4)
         fill(9, 0)
-        square(0, 0, 5)
-        scale_gr(9, (0, 1))
         fill(8, 0)
-        fill(9, 1)
+        combine(4, (0,))
+        scale_c_planar(3, 0, 4)
+        interleave_h(1)
+        combine(4, (1,))
+        combine(5, (0,))
+        combine(5, (1,))
+        fill(6, 1)
+        fill(7, 1)
+        scale_gr(9, (0,))
+        scale_gr(8, (1,))
+        quantize_h(1)
+        quantize_c(2, 1)
+        combine(6, (0,))
+        scale_gr(8, (0,))
+        combine(7, (0,))
         loop_gain(0, 1, 6, (0, 1))
-        combine(6)
-        square(0, 1, 6)
-        add_identity(0, 0, 5)
-        loop_gain(0, 3, 5, (0, 1))
-        loop_gain(0, 2, 7, (0, 1))
+        loop_gain(0, 0, 5, (0, 1))
+        interleave_c(3, 0, "A")
         interleave_h(2)
+        loop_gain(0, 3, 4, (0, 1))
+        scale_gr(9, (1,))
+        loop_gain(0, 2, 7, (0, 1))
+        fill(10, 0)
+        add_identity(0, 1, 6)
+        combine(7, (1,))
+        add_identity(0, 0, 5)
+        fill(9, 1)
+        add_identity(0, 3, 4)
+        square(0, 0, 5)
+        combine(6, (1,))
+        add_identity(0, 2, 7)
+        quantize_h(2)
+        square(0, 1, 6)
+        interleave_h(3)
+        square(0, 2, 7)
+        square(0, 3, 4)
+        quantize_c(3, 0)
         fill(8, 1)
         fill(11, 0)
-        scale_c(3, 1, 4)
-        quantize_h(2)
-        add_identity(0, 1, 6)
-        add_identity(0, 3, 5)
-        add_identity(0, 2, 7)
-        scale_gr(8, (0, 1))
-        scale_gr(11, (0,))
-        square_diagonal(0, 0)
-        combine(9)
-        square(0, 2, 7)
-        square(0, 3, 5)
-        interleave_h(3)
-        fill(11, 1)
-        sum_squares(0, 0, 6)
-        scale_c(3, 0, 4)
-        scale_gr_vector(11, 1)
-        combine(8)
-        square_diagonal(0, 1)
-        root(0, 0, 6)
-        store_root(0, 0)
-        fill(10, 0)
+        sum_squares(0, 0, 2, 5)
+        combine(9, (0,))
+        scale_gr(10, (1,))
+        combine(8, (1,))
+        combine(8, (0,))
+        combine(9, (1,))
+        scale_gr(10, (0,))
+        root(0, 0, 2, 5)
+        store_root(0, 0, 2)
+        sum_squares(0, 2, 2, 6)
         quantize_h(3)
-        loop_gain(1, 0, 5, (0, 1))
         fill(10, 1)
-        quantize_c(3, 0)
-        combine(11)
-        scale_gr(10, (0, 1))
-        square(1, 0, 5)
-        fill(13, 0)
-        loop_gain(1, 1, 6, (0, 1))
-        combine(10)
-        add_identity(1, 1, 6)
-        add_identity(1, 0, 5)
-        fill(12, 0)
-        scale_gr(13, (0,))
-        sum_squares(0, 1, 7)
+        scale_gr(11, (1,))
+        scale_gr(11, (0,))
         quantize_c(3, 1)
+        fill(11, 1)
+        fill(12, 0)
+        combine(10, (1,))
+        loop_gain(1, 0, 7, (0, 1))
+        root(0, 2, 2, 6)
+        store_root(0, 2, 2)
+        scale_gr(12, (1,))
         interleave_h(4)
-        quantize_h(4)
-        square(1, 1, 6)
-        square_diagonal(1, 0)
-        fill(13, 1)
-        root(0, 1, 7)
-        store_root(0, 1)
-        loop_gain(1, 3, 5, (0, 1))
-        fill(12, 1)
-        scale_gr_vector(13, 1)
-        interleave_h(5)
-        scale_gr(12, (0, 1))
-        fill(15, 0)
-        loop_gain(1, 2, 7, (0, 1))
-        square(1, 3, 5)
-        combine(13)
-        combine(12)
-        add_identity(1, 2, 7)
-        quantize_h(5)
-        add_identity(1, 3, 5)
-        scale_gr(15, (0,))
+        add_identity(1, 0, 7)
+        combine(11, (0,))
+        loop_gain(1, 1, 4, (0, 1))
+        combine(11, (1,))
+        add_identity(1, 1, 4)
+        loop_gain(1, 2, 5, (0, 1))
+        loop_gain(1, 3, 6, (0, 1))
+        square(1, 0, 7)
+        combine(10, (0,))
+        fill(13, 0)
+        add_identity(1, 2, 5)
+        add_identity(1, 3, 6)
+        scale_gr(12, (0,))
         fill(14, 0)
-        scale_gr(14, (0, 1))
-        interleave_h(6)
+        fill(13, 1)
+        quantize_h(4)
+        fill(12, 1)
+        interleave_h(5)
+        square(1, 1, 4)
+        combine(12, (0,))
+        square(1, 2, 5)
+        combine(12, (1,))
+        sum_squares(1, 0, 2, 7)
+        square(1, 3, 6)
+        scale_gr(13, (0,))
+        scale_gr(13, (1,))
+        sum_squares(1, 2, 2, 4)
+        fill(15, 0)
+        combine(13, (0,))
+        combine(13, (1,))
+        scale_gr(14, (1,))
+        root(1, 0, 2, 7)
+        store_root(1, 0, 2)
+        scale_gr(14, (0,))
         fill(14, 1)
-        combine(14)
-        sum_squares(1, 0, 6)
-        loop_gain(2, 0, 5, (0, 1))
-        scale_gr_vector(15, 1)
+        scale_gr(15, (0,))
         fill(15, 1)
-        square(1, 2, 7)
-        square_diagonal(1, 1)
-        root(1, 0, 6)
-        store_root(1, 0)
-        add_identity(2, 0, 5)
-        square(2, 0, 5)
-        combine(15)
-        quantize_h(6)
-        sum_squares(1, 1, 7)
+        quantize_h(5)
+        scale_gr(15, (1,))
+        interleave_h(6)
+        root(1, 2, 2, 4)
+        store_root(1, 2, 2)
+        combine(14, (0,))
+        loop_gain(2, 0, 5, (0, 1))
         loop_gain(2, 1, 6, (0, 1))
-        loop_gain(2, 3, 5, (0, 1))
-        add_identity(2, 1, 6)
-        loop_gain(3, 3, 2, (0,))
-        loop_gain(3, 1, 0, (0,))
-        square(2, 1, 6)
-        interleave_h_vector(7)
-        quantize_h(7)
-        loop_gain(3, 0, 4, (0,))
-        root(1, 1, 7)
-        store_root(1, 1)
-        loop_gain(3, 2, 1, (0,))
-        square_diagonal(2, 0)
+        add_identity(2, 0, 5)
+        combine(15, (0,))
         loop_gain(2, 2, 7, (0, 1))
-        loop_gain(3, 0, 4, (1,))
-        loop_gain(3, 1, 0, (1,))
-        loop_gain(3, 3, 2, (1,))
-        loop_gain(3, 2, 1, (1,))
-        square(2, 3, 5)
-        square(2, 2, 7)
-        round_result(0, 1, "G")
-        add_identity(2, 3, 5)
-        add_identity(3, 1, 0)
+        square(2, 0, 5)
+        add_identity(2, 1, 6)
+        square(2, 1, 6)
+        combine(15, (1,))
         add_identity(2, 2, 7)
-        square(3, 0, 4)
-        sum_squares(2, 0, 6)
-        square(3, 1, 0)
-        add_identity(3, 2, 1)
-        add_identity(3, 0, 4)
-        square_diagonal(2, 1)
-        round_result(0, 0, "G")
-        square_diagonal(3, 0)
-        add_identity(3, 3, 2)
-        sum_squares(3, 0, 5)
-        quantize_result(0, 0, 512)
-        store_codes(0, 0, 512)
-        square(3, 2, 1)
-        square(3, 3, 2)
-        sum_squares(2, 1, 7)
-        square_diagonal(3, 1)
-        sum_squares(3, 1, 3)
-        root(2, 0, 6)
-        store_root(2, 0)
-        root(3, 0, 5)
-        store_root(3, 0)
-        root(2, 1, 7)
-        store_root(2, 1)
-        round_result(1, 0, "V")
-        quantize_result(1, 0, 256)
-        store_codes(1, 0, 256)
-        root(3, 1, 3)
-        store_root(3, 1)
-        round_result(1, 1, "V")
-        quantize_result(1, 256, 512)
-        store_codes(1, 256, 512)
+        combine(14, (1,))
+        quantize_h(6)
+        loop_gain(2, 3, 4, (0, 1))
+        sum_squares(2, 0, 2, 5)
+        square(2, 2, 7)
+        square(2, 3, 4)
+        interleave_h_part(7, 0, "V")
+        interleave_h_part(7, 1, "V")
+        add_identity(2, 3, 4)
+        quantize_h_part(7, 0)
+        quantize_h_part(7, 1)
+        sum_squares(2, 2, 1, 6)
+        loop_gain(3, 2, 2, (0,))
+        loop_gain(3, 0, 0, (0,))
+        loop_gain(3, 1, 1, (0,))
+        loop_gain(3, 3, 4, (0,))
+        loop_gain(3, 0, 0, (1,))
+        root(2, 0, 2, 5)
+        store_root(2, 0, 2)
+        loop_gain(3, 1, 1, (1,))
+        loop_gain(3, 2, 2, (1,))
+        root(2, 2, 1, 6)
+        store_root(2, 2, 1)
+        loop_gain(3, 3, 4, (1,))
+        square(3, 0, 0)
+        round_result(0, 0, 2, "V")
+        round_result(0, 2, 2, "V")
+        add_identity(3, 1, 1)
+        add_identity(3, 0, 0)
+        sum_squares(2, 3, 1, 7)
+        add_identity(3, 2, 2)
+        square(3, 1, 1)
+        sum_squares(3, 0, 2, 3)
+        square(3, 3, 4)
+        square(3, 2, 2)
+        quantize_result(0, 2, 2)
+        store_codes(0, 2, 2)
+        add_identity(3, 3, 4)
+        quantize_result(0, 0, 2)
+        store_codes(0, 0, 2)
+        root(2, 3, 1, 7)
+        store_root(2, 3, 1)
+        sum_squares(3, 3, 1, 6)
+        root(3, 0, 2, 3)
+        store_root(3, 0, 2)
+        round_result(1, 0, 2, "V")
+        root(3, 3, 1, 6)
+        store_root(3, 3, 1)
+        sum_squares(3, 2, 1, 5)
+        root(3, 2, 1, 5)
+        store_root(3, 2, 1)
+        round_result(1, 3, 1, "V")
+        round_result(1, 2, 1, "V")
+        quantize_result(1, 0, 2)
+        store_codes(1, 0, 2)
+        quantize_result(1, 3, 1)
+        store_codes(1, 3, 1)
+        quantize_result(1, 2, 1)
+        store_codes(1, 2, 1)
         store_scales()

@@ -40,7 +40,6 @@ def tile_delayedmodalloopreturndifferencemagnitud_x2_kernel(
             return sb.tile(shape, dtype, name=name, align_bytes=64)
 
         banks = [ps.tile([PARTS, 512], F32, name="bank%d" % i) for i in range(8)]
-        gr_banks, gi_banks = banks[0:2], banks[2:4]
 
         alpha_sb = sbuf("alpha_sb", [PARTS, PACK], BF16)
         beta_sb = sbuf("beta_sb", [PARTS, PACK], BF16)
@@ -108,7 +107,7 @@ def tile_delayedmodalloopreturndifferencemagnitud_x2_kernel(
 
         def store_scales():
             for q in range(4):
-                nc.sync.dma_start(
+                (nc.sync, nc.scalar)[q % 2].dma_start(
                     out=out_2[0, 4 * q : 4 * q + 4, :].bitcast(I32),
                     in_=out_scales[32 * q : 32 * q + 4, :].bitcast(I32),
                 )
@@ -127,7 +126,8 @@ def tile_delayedmodalloopreturndifferencemagnitud_x2_kernel(
         fabs = sbuf("fabs", [PARTS, W * 8], F32)
         co = sbuf("co", [PARTS, W * 8], F32)
         si = sbuf("si", [PARTS, W * 8], F32)
-        nsi = sbuf("nsi", [PARTS, W * 8], F32)
+        on_gi = sbuf("on_gi", [PARTS, W * 8], F32)
+        on_gr = sbuf("on_gr", [PARTS, W * 8], F32)
 
         def over_w(t):
             return t[:].unsqueeze(1).to_broadcast([PARTS, W, PACK])
@@ -179,9 +179,14 @@ def tile_delayedmodalloopreturndifferencemagnitud_x2_kernel(
 
         def sines():
             nc.scalar.activation(out=si[:], in_=frac[:], func=ACT.Sin, scale=2.0 * math.pi)
-            nc.scalar.activation(out=nsi[:], in_=frac[:], func=ACT.Sin, scale=-2.0 * math.pi)
             nc.scalar.activation(out=co[:], in_=fabs[:], func=ACT.Sin, scale=-2.0 * math.pi, bias=0.5 * math.pi)
             nc.scalar.activation(out=warm2[:], in_=warm[:, 0:1], func=ACT.Sqrt)
+
+        def delay_factors():
+            nc.vector.tensor_tensor(out=on_gi[:], in0=si[:], in1=co[:], op=ALU.subtract)
+            nc.vector.scalar_tensor_tensor(
+                out=on_gr[:], in0=si[:], scalar=-1.0, in1=co[:], op0=ALU.mult, op1=ALU.subtract
+            )
 
         def permute_b_words(g):
             nc.vector.tensor_copy(
@@ -194,17 +199,17 @@ def tile_delayedmodalloopreturndifferencemagnitud_x2_kernel(
                 out=bs[:, g, :, :], in_=bs_raw[:, 512 * g : 512 * (g + 1)].rearrange("p (q t) -> p t q", t=PACK)
             )
 
-        crb = [sbuf("crb%d" % i, [PARTS, PACK * HALF], BF16) for i in range(2 * UNITS)]
-        crq = [sbuf("crq%d" % i, [PARTS, HALF], U32) for i in range(2 * UNITS)]
-        crs = [sbuf("crs%d" % i, [PARTS, HALF], U8) for i in range(2 * UNITS)]
+        crb = [sbuf("crb%d" % i, [PARTS, PACK * HALF], BF16) for i in range(6)]
+        crq = [sbuf("crq%d" % i, [PARTS, P], U32) for i in range(2 * W)]
+        crs = [sbuf("crs%d" % i, [PARTS, P], U8) for i in range(2 * W)]
 
-        crp = [sbuf("crp%d" % i, [PARTS, PACK, HALF], BF16) for i in range(8)]
+        crp = [sbuf("crp%d" % i, [PARTS, PACK, HALF], BF16) for i in range(4)]
 
         def scale_c_planar(u, ri, b):
             bank = banks[b]
             for j in range(PACK):
                 nc.scalar.activation(
-                    out=crp[2 * u + ri][:, j, :],
+                    out=crp[(2 * u + ri) % 4][:, j, :],
                     in_=bank[:].bitcast(BF16).rearrange("p (a n e) -> p a e n", a=2, e=2)[:, j // 2, j % 2, :],
                     func=ACT.Copy,
                     scale=dfac[ri][:, u // 2, j : j + 1],
@@ -212,11 +217,13 @@ def tile_delayedmodalloopreturndifferencemagnitud_x2_kernel(
 
         def interleave_c(u, ri, eng):
             out = crb[CRB[2 * u + ri]][:].rearrange("p (n t) -> p n t", t=PACK)
-            in_ = crp[2 * u + ri][:].rearrange("p t n -> p n t")
+            in_ = crp[(2 * u + ri) % 4][:].rearrange("p t n -> p n t")
             if eng == "G":
                 nc.gpsimd.tensor_scalar(out=out, in0=in_, scalar1=1.0, scalar2=0.0, op0=ALU.mult, op1=ALU.add)
             else:
-                nc.scalar.copy(out=out, in_=in_)
+                nc.scalar.copy(
+                    out=out.rearrange("p (c i) t -> p c t i", i=4), in_=in_.rearrange("p (c i) t -> p c t i", i=4)
+                )
 
         def transpose_c(u, b):
             words = c_sb[u % 2][:].bitcast(F32)
@@ -237,65 +244,105 @@ def tile_delayedmodalloopreturndifferencemagnitud_x2_kernel(
             )
 
         def quantize_c(u, ri):
-            i = 2 * u + ri
-            nc.vector.quantize_mx(out=crq[i][:].bitcast(FP8X4), scales=crs[i][:], in_=crb[CRB[i]][:])
+            i = 2 * (u // 2) + ri
+            cols = slice(HALF * (u % 2), HALF * (u % 2 + 1))
+            nc.vector.quantize_mx(
+                out=crq[i][:, cols].bitcast(FP8X4), scales=crs[i][:, cols], in_=crb[CRB[2 * u + ri]][:]
+            )
 
-        def fill(h, ri):
-            u, g, j = h // 4, (h // 2) % 2, h % 2
-            bank = (gr_banks, gi_banks)[ri][h % 2]
+        def plant_pass(out, g, t, i, cols, start, stop):
+            nc.tensor.matmul_mx(
+                out=out,
+                lhsT=bw[:, g, t, :].bitcast(FP4X4),
+                lhsT_scale=bs[:, g, t, :],
+                rhs=crq[i][:, cols].bitcast(FP8X4),
+                rhs_scale=crs[i][:, cols],
+                start=start,
+                stop=stop,
+            )
+
+        def fill(u, g, t, b):
+            cols = slice(HALF * (u % 2), HALF * (u % 2 + 1))
+            for ri in range(2):
+                plant_pass(banks[b][:, HALF * ri : HALF * (ri + 1)], g, t, 2 * (u // 2) + ri, cols, True, True)
+
+        def fill_sum(w, g, t, b):
+            for ri in range(2):
+                plant_pass(banks[b][:], g, t, 2 * w + ri, slice(0, P), ri == 0, ri == 1)
+
+        def fill_sum_narrow(u, g, t, b):
             for tl in range(2):
-                t = 2 * j + tl
-                nc.tensor.matmul_mx(
-                    out=bank[:, HALF * tl : HALF * (tl + 1)],
-                    lhsT=bw[:, g, t, :].bitcast(FP4X4),
-                    lhsT_scale=bs[:, g, t, :],
-                    rhs=crq[2 * u + ri][:].bitcast(FP8X4),
-                    rhs_scale=crs[2 * u + ri][:],
-                    start=True,
-                    stop=True,
-                )
+                for k in range(2):
+                    cols = slice(HALF * (u % 2) + PARTS * k, HALF * (u % 2) + PARTS * (k + 1))
+                    dst = HALF * tl + PARTS * k
+                    for ri in range(2):
+                        plant_pass(
+                            banks[b][:, dst : dst + PARTS], g, t + tl, 2 * (u // 2) + ri, cols, ri == 0, ri == 1
+                        )
 
-        part = [sbuf("part%d" % i, [PARTS, 2, 2, HALF], F32) for i in range(4)]
+        shared = [sbuf("shared%d" % i, [PARTS, P], F32) for i in range(8)]
         hpl = [sbuf("hpl%d" % i, [PARTS, 2, PACK, HALF], BF16) for i in range(3)]
         hil = sbuf("hil", [PARTS, 2, HALF, PACK], BF16)
+        hil2 = [sbuf("hil2_%d" % i, [PARTS, HALF, PACK], BF16) for i in range(2)]
         hq = [sbuf("hq%d" % i, [PARTS, 2 * HALF], U32) for i in range(2 * UNITS)]
         hs = [sbuf("hs%d" % i, [PARTS, 2 * HALF], U8) for i in range(2 * UNITS)]
 
-        def factor(tile, h, tl):
-            col = 8 * (h // 8) + PACK * ((h // 2) % 2) + 2 * (h % 2) + tl
+        def factor(tile, w, g, t):
+            col = 8 * w + PACK * g + t
             return tile[:, col : col + 1]
 
-        def scale_gr(h, tls=(0, 1)):
-            for tl in tls:
-                for ri in range(2):
-                    nc.scalar.activation(
-                        out=part[h % 4][:, tl, ri, :],
-                        in_=gr_banks[h % 2][:, HALF * tl : HALF * (tl + 1)],
-                        func=ACT.Copy,
-                        scale=factor((co, nsi)[ri], h, tl),
-                    )
+        def scale_sum(w, g, t, b):
+            nc.scalar.activation(
+                out=shared[PACK * g + t][:], in_=banks[b][:], func=ACT.Copy, scale=factor(co, w, g, t)
+            )
 
-        def scale_gr_vector(h, tl):
+        def scale_sum_narrow(u, g, t, tl, b):
+            w = u // 2
+            nc.scalar.activation(
+                out=part[PACK * g + t + tl][:, 0, :],
+                in_=banks[b][:, HALF * tl : HALF * (tl + 1)],
+                func=ACT.Copy,
+                scale=factor(co, w, g, t + tl),
+            )
+
+        def combine(u, g, t, b):
+            w = u // 2
             for ri in range(2):
-                nc.vector.tensor_scalar(
-                    out=part[h % 4][:, tl, ri, :],
-                    in0=gr_banks[h % 2][:, HALF * tl : HALF * (tl + 1)],
-                    scalar1=factor((co, nsi)[ri], h, tl),
-                    scalar2=None,
+                nc.vector.scalar_tensor_tensor(
+                    out=hpl[(2 * u + g) % 3][:, ri, t, :],
+                    in0=banks[b][:, HALF * (1 - ri) : HALF * (2 - ri)],
+                    scalar=factor((on_gi, on_gr)[ri], w, g, t),
+                    in1=shared[PACK * g + t][:, HALF * (u % 2) : HALF * (u % 2 + 1)] if w else part[PACK * g + t][:, 0, :],
                     op0=ALU.mult,
+                    op1=ALU.add,
                 )
 
-        def combine(h, tls):
-            for tl in tls:
-                for ri in range(2):
-                    nc.vector.scalar_tensor_tensor(
-                        out=hpl[(h // 2) % 3][:, ri, 2 * (h % 2) + tl, :],
-                        in0=gi_banks[h % 2][:, HALF * tl : HALF * (tl + 1)],
-                        scalar=factor((si, co)[ri], h, tl),
-                        in1=part[h % 4][:, tl, ri, :],
-                        op0=ALU.mult,
-                        op1=ALU.add,
-                    )
+        part = [sbuf("part%d" % i, [PARTS, 2, HALF], F32) for i in range(8)]
+
+        def fill_pair(u, g, j, ri, b):
+            cols = slice(HALF * (u % 2), HALF * (u % 2 + 1))
+            for tl in range(2):
+                plant_pass(banks[b][:, HALF * tl : HALF * (tl + 1)], g, 2 * j + tl, 2 * (u // 2) + ri, cols, True, True)
+
+        def scale_gr(u, g, t, b):
+            for ri in range(2):
+                nc.scalar.activation(
+                    out=part[PACK * g + t][:, ri, :],
+                    in_=banks[b][:, HALF * (t % 2) : HALF * (t % 2 + 1)],
+                    func=ACT.Copy,
+                    scale=factor((co, si)[ri], u // 2, g, t),
+                )
+
+        def combine_gi(u, g, t, b):
+            for ri in range(2):
+                nc.vector.scalar_tensor_tensor(
+                    out=hpl[(2 * u + g) % 3][:, ri, t, :],
+                    in0=banks[b][:, HALF * (t % 2) : HALF * (t % 2 + 1)],
+                    scalar=factor((si, co)[ri], u // 2, g, t),
+                    in1=part[PACK * g + t][:, ri, :],
+                    op0=ALU.mult,
+                    op1=(ALU.add, ALU.subtract)[ri],
+                )
 
         def interleave_h(s):
             nc.gpsimd.tensor_scalar(
@@ -312,7 +359,29 @@ def tile_delayedmodalloopreturndifferencemagnitud_x2_kernel(
                 out=hq[s][:].bitcast(FP8X4), scales=hs[s][:], in_=hil[:].rearrange("p r n t -> p (r n t)")
             )
 
-        sq = [sbuf("sq%d" % i, [PARTS, 4 * 512], F32) for i in range(2)]
+        def part_buffer(s, ri, eng):
+            return hil2[(s + ri) % 2][:] if eng == "A" else hil[:, ri, :, :]
+
+        def interleave_h_part(s, ri, eng):
+            out = part_buffer(s, ri, eng)
+            in_ = hpl[s % 3][:, ri, :, :]
+            if eng == "G":
+                nc.gpsimd.tensor_scalar(
+                    out=out, in0=in_.rearrange("p t n -> p n t"), scalar1=1.0, scalar2=0.0, op0=ALU.mult, op1=ALU.add
+                )
+            else:
+                copy = nc.scalar.copy if eng == "A" else nc.vector.tensor_copy
+                copy(out=out.rearrange("p (c i) t -> p c t i", i=4), in_=in_.rearrange("p t (c i) -> p c t i", i=4))
+
+        def quantize_h_part(s, ri, eng):
+            cols = slice(HALF * ri, HALF * (ri + 1))
+            nc.vector.quantize_mx(
+                out=hq[s][:, cols].bitcast(FP8X4),
+                scales=hs[s][:, cols],
+                in_=part_buffer(s, ri, eng).rearrange("p n t -> p (n t)"),
+            )
+
+        sq = [sbuf("sq%d" % i, [PARTS, 4 * 544], F32) for i in range(2)]
         res = {
             (w, j0): sbuf("res%d_%d" % (w, j0), [PARTS, PACK, PARTS * nj], F32)
             for w in range(W)
@@ -339,16 +408,6 @@ def tile_delayedmodalloopreturndifferencemagnitud_x2_kernel(
             bank = banks[b]
             nc.scalar.activation(out=sq[u % 2][:, 512 * j : 512 * (j + 1)], in_=bank[:], func=ACT.Square)
 
-        raw = [sbuf("raw%d" % i, [PARTS, 512], F32) for i in range(4)]
-
-        def copy_gain(u, j, b):
-            nc.vector.tensor_copy(out=raw[j][:], in_=banks[b][:])
-
-        def square_vector(u, j):
-            nc.vector.tensor_tensor(
-                out=sq[u % 2][:, 512 * j : 512 * (j + 1)], in0=raw[j][:], in1=raw[j][:], op=ALU.mult
-            )
-
         def add_identity(u, j, b):
             t0 = 2 * (u % 2)
             nc.vector.scalar_tensor_tensor(
@@ -360,7 +419,26 @@ def tile_delayedmodalloopreturndifferencemagnitud_x2_kernel(
                 op1=ALU.mult,
             )
 
-        def sum_squares(u, j0, nj, b):
+        diag = [sbuf("diag%d" % i, [PARTS, 4, 2, 32], F32) for i in range(2)]
+
+        def add_one(u, j, b):
+            t0 = 2 * (u % 2)
+            nc.vector.tensor_tensor(
+                out=diag[u % 2][:, j, :, :],
+                in0=banks[b][:, 0:HALF].rearrange("p (t q) -> p t q", t=2)[:, :, 32 * j : 32 * (j + 1)],
+                in1=ident[:].rearrange("p (q t) -> p t q", t=PACK)[:, t0 : t0 + 2, :],
+                op=ALU.add,
+            )
+
+        def square_diagonal(u, j0, nj):
+            blocks = sq[u % 2][:].rearrange("p (j s) -> p j s", s=544)[:, j0 : j0 + nj, 0:HALF]
+            nc.scalar.activation(
+                out=blocks.rearrange("p j (t q) -> p j t q", t=2)[:, :, :, 0:32],
+                in_=diag[u % 2][:, j0 : j0 + nj, :, :],
+                func=ACT.Square,
+            )
+
+        def sum_squares(u, j0, nj, b, nterms):
             for tl in range(2):
                 for jl in range(nj):
                     j = j0 + jl
@@ -371,13 +449,13 @@ def tile_delayedmodalloopreturndifferencemagnitud_x2_kernel(
                         cross[:, j, tl, :],
                     )
                     dst = PARTS * (nj * tl + jl)
-                    for i, term in enumerate(terms):
+                    for i, term in enumerate(terms[:nterms]):
                         nc.tensor.matmul(
                             out=banks[b][:, dst : dst + PARTS],
                             lhsT=term,
                             rhs=ident[:],
                             start=(i == 0),
-                            stop=(i == 2),
+                            stop=(i == nterms - 1),
                             is_transpose=True,
                         )
 
@@ -403,10 +481,9 @@ def tile_delayedmodalloopreturndifferencemagnitud_x2_kernel(
             in_ = res[w, j0][:].rearrange("p t n -> p n t")
             if eng == "G":
                 nc.gpsimd.tensor_scalar(out=out, in0=in_, scalar1=1.0, scalar2=0.0, op0=ALU.mult, op1=ALU.add)
-            elif eng == "A":
-                nc.scalar.copy(out=out, in_=in_)
             else:
-                nc.vector.tensor_copy(out=out, in_=in_)
+                copy = nc.scalar.copy if eng == "A" else nc.vector.tensor_copy
+                copy(out=out.rearrange("p (c i) t -> p c t i", i=4), in_=in_.rearrange("p (c i) t -> p c t i", i=4))
 
         def quantize_result(w, j0, nj):
             cols = slice(P * w + PARTS * j0, P * w + PARTS * (j0 + nj))
@@ -422,292 +499,276 @@ def tile_delayedmodalloopreturndifferencemagnitud_x2_kernel(
                 out=out_1[0].rearrange("p n t -> p (n t)").bitcast(I32)[:, cols], in_=out_codes[:, cols].bitcast(I32)
             )
 
-        ct_sb = [sbuf("ct_sb%d" % i, [PARTS, HALF, PACK], BF16) for i in range(2)]
-
-        def copy_ct(half, b):
-            nc.scalar.copy(out=ct_sb[half][:].bitcast(F32), in_=banks[b][:].rearrange("p (a n) -> p n a", a=2))
-
-        def scale_c_gpsimd(u, ri):
-            nc.gpsimd.tensor_tensor(
-                out=crb[CRB[2 * u + ri]][:].rearrange("p (n t) -> p n t", t=PACK),
-                in0=ct_sb[u % 2][:],
-                in1=dfac[ri][:, u // 2, :].unsqueeze(1).to_broadcast([PARTS, HALF, PACK]),
-                op=ALU.mult,
-            )
-
-        def interleave_h_part(s, ri, eng):
-            out = hil[:, ri, :, :]
-            in_ = hpl[s % 3][:, ri, :, :].rearrange("p t n -> p n t")
-            if eng == "A":
-                nc.scalar.copy(out=out, in_=in_)
-            else:
-                nc.vector.tensor_copy(out=out, in_=in_)
-
-        def quantize_h_part(s, ri):
-            cols = slice(HALF * ri, HALF * (ri + 1))
-            nc.vector.quantize_mx(
-                out=hq[s][:, cols].bitcast(FP8X4),
-                scales=hs[s][:, cols],
-                in_=hil[:, ri, :, :].rearrange("p n t -> p (n t)"),
-            )
-
-        def interleave_h_vector(s):
-            nc.vector.tensor_copy(out=hil[:], in_=hpl[s % 3][:].rearrange("p r t n -> p r n t"))
-
-        clear_first()
-        load_matrices()
         identity()
+        clear_first()
         load_vectors()
-        spread_omega(6)
-        resolvent(0)
+        load_matrices()
         permute_b_words(0)
+        spread_omega(6)
         copy_omega(6)
-        phase(0)
+        resolvent(0)
+        permute_b_scales(1)
         resolvent(1)
-        transpose_c(0, 4)
+        phase(0)
         resolvent(2)
         phase(1)
         resolvent(3)
         phase(2)
         resolvent(4)
-        phase(3)
-        permute_b_scales(1)
-        phase(4)
         transpose_c(0, 5)
-        scale_c(0, 0, 4)
-        scale_c(0, 1, 4)
-        transpose_c(1, 4)
-        clear_cross()
-        quantize_c(0, 0)
+        transpose_c(0, 4)
+        phase(3)
         permute_b_scales(0)
-        quantize_c(0, 1)
         scale_c_planar(2, 0, 5)
-        phase(5)
+        phase(4)
+        scale_c(0, 1, 4)
+        scale_c(0, 0, 4)
         permute_b_words(1)
-        fill(0, 0)
-        scale_c_planar(2, 1, 5)
-        fill(0, 1)
-        sines()
+        quantize_c(0, 0)
+        transpose_c(1, 4)
+        fill_pair(0, 0, 0, 0, 2)
+        fill_pair(0, 0, 1, 0, 3)
+        quantize_c(0, 1)
         scale_c(1, 0, 4)
-        fill(1, 0)
-        scale_gr(0, (1,))
-        scale_gr(0, (0,))
-        fill(1, 1)
-        scale_gr(1, (1,))
-        combine(0, (1,))
-        interleave_c(2, 0, "G")
-        combine(0, (0,))
-        scale_gr(1, (0,))
-        combine(1, (1,))
-        fill(2, 0)
-        combine(1, (0,))
-        fill(3, 0)
-        quantize_c(1, 0)
-        fill(2, 1)
-        interleave_c(2, 1, "G")
-        scale_c(1, 1, 4)
-        scale_gr(2, (1,))
-        scale_gr(2, (0,))
-        fill(3, 1)
-        fill(4, 0)
-        combine(2, (1,))
-        scale_gr(3, (1,))
-        scale_gr(3, (0,))
-        interleave_h(0)
-        fill(5, 0)
-        scale_gr(4, (0,))
-        scale_gr(4, (1,))
-        combine(2, (0,))
-        fill(6, 0)
-        combine(3, (0,))
-        combine(3, (1,))
-        scale_gr(5, (0,))
-        quantize_c(1, 1)
-        scale_gr(5, (1,))
-        scale_gr(6, (0,))
-        quantize_h(0)
-        fill(4, 1)
-        quantize_c(2, 0)
-        scale_gr(6, (1,))
-        fill(7, 0)
-        fill(5, 1)
-        scale_gr(7, (1,))
-        scale_gr(7, (0,))
+        phase(5)
+        scale_c_planar(2, 1, 5)
         scale_c(3, 1, 4)
-        fill(9, 0)
-        fill(8, 0)
-        combine(4, (0,))
+        sines()
+        scale_gr(0, 0, 1, 2)
+        fill_pair(0, 0, 0, 1, 0)
+        scale_gr(0, 0, 0, 2)
+        scale_gr(0, 0, 2, 3)
+        fill_pair(0, 0, 1, 1, 1)
         scale_c_planar(3, 0, 4)
-        interleave_h(1)
-        combine(4, (1,))
-        combine(5, (0,))
-        combine(5, (1,))
-        fill(6, 1)
-        fill(7, 1)
-        scale_gr(9, (0,))
-        scale_gr(8, (1,))
-        quantize_h(1)
-        quantize_c(2, 1)
-        combine(6, (0,))
-        scale_gr(8, (0,))
-        combine(7, (0,))
-        loop_gain(0, 1, 6, (0, 1))
-        loop_gain(0, 0, 5, (0, 1))
+        combine_gi(0, 0, 1, 0)
+        combine_gi(0, 0, 0, 0)
+        delay_factors()
+        interleave_c(2, 1, "G")
+        fill_pair(0, 1, 0, 0, 2)
+        combine_gi(0, 0, 2, 1)
+        scale_gr(0, 0, 3, 3)
+        fill_pair(0, 1, 1, 0, 3)
+        fill_pair(0, 1, 0, 1, 0)
         interleave_c(3, 0, "A")
-        interleave_h(2)
-        loop_gain(0, 3, 4, (0, 1))
-        scale_gr(9, (1,))
-        loop_gain(0, 2, 7, (0, 1))
-        fill(10, 0)
-        add_identity(0, 1, 6)
-        combine(7, (1,))
-        add_identity(0, 0, 5)
-        fill(9, 1)
-        add_identity(0, 3, 4)
-        square(0, 0, 5)
-        combine(6, (1,))
-        add_identity(0, 2, 7)
-        quantize_h(2)
-        square(0, 1, 6)
-        interleave_h(3)
-        square(0, 2, 7)
-        square(0, 3, 4)
-        quantize_c(3, 0)
-        fill(8, 1)
-        fill(11, 0)
-        sum_squares(0, 0, 2, 5)
-        combine(9, (0,))
-        scale_gr(10, (1,))
-        combine(8, (1,))
-        combine(8, (0,))
-        combine(9, (1,))
-        scale_gr(10, (0,))
-        root(0, 0, 2, 5)
-        store_root(0, 0, 2)
-        sum_squares(0, 2, 2, 6)
-        quantize_h(3)
-        fill(10, 1)
-        scale_gr(11, (1,))
-        scale_gr(11, (0,))
+        interleave_c(2, 0, "G")
         quantize_c(3, 1)
-        fill(11, 1)
-        fill(12, 0)
-        combine(10, (1,))
-        loop_gain(1, 0, 7, (0, 1))
-        root(0, 2, 2, 6)
+        combine_gi(0, 0, 3, 1)
+        quantize_c(2, 1)
+        fill_pair(0, 1, 1, 1, 1)
+        scale_gr(0, 1, 1, 2)
+        quantize_c(1, 0)
+        scale_gr(0, 1, 3, 3)
+        quantize_c(2, 0)
+        quantize_c(3, 0)
+        scale_gr(0, 1, 2, 3)
+        scale_gr(0, 1, 0, 2)
+        scale_c(1, 1, 4)
+        fill_sum(1, 0, 0, 6)
+        fill_sum(1, 0, 1, 7)
+        interleave_h(0)
+        scale_sum(1, 0, 0, 6)
+        combine_gi(0, 1, 1, 0)
+        fill_pair(1, 0, 0, 0, 2)
+        fill_pair(1, 0, 1, 0, 3)
+        combine_gi(0, 1, 2, 1)
+        scale_sum(1, 0, 1, 7)
+        scale_gr(1, 0, 0, 2)
+        combine_gi(0, 1, 0, 0)
+        scale_gr(1, 0, 1, 2)
+        combine_gi(0, 1, 3, 1)
+        fill_sum(1, 0, 2, 6)
+        fill_sum(1, 0, 3, 7)
+        scale_sum(1, 0, 2, 6)
+        scale_gr(1, 0, 3, 3)
+        scale_gr(1, 0, 2, 3)
+        quantize_c(1, 1)
+        quantize_h(0)
+        fill_pair(1, 0, 0, 1, 0)
+        fill_pair(1, 0, 1, 1, 1)
+        fill_pair(1, 1, 0, 0, 2)
+        combine_gi(1, 0, 1, 0)
+        fill_sum(1, 1, 0, 6)
+        scale_sum(1, 0, 3, 7)
+        combine_gi(1, 0, 0, 0)
+        fill_pair(1, 1, 1, 0, 3)
+        combine_gi(1, 0, 2, 1)
+        scale_sum(1, 1, 0, 6)
+        combine_gi(1, 0, 3, 1)
+        interleave_h(1)
+        scale_gr(1, 1, 0, 2)
+        fill_pair(1, 1, 0, 1, 0)
+        fill_sum(1, 1, 1, 7)
+        scale_gr(1, 1, 1, 2)
+        quantize_h(1)
+        fill_pair(1, 1, 1, 1, 1)
+        fill_sum(1, 1, 2, 6)
+        combine_gi(1, 1, 0, 0)
+        scale_gr(1, 1, 2, 3)
+        combine_gi(1, 1, 1, 0)
+        scale_gr(1, 1, 3, 3)
+        loop_gain(0, 1, 4, (0, 1))
+        combine_gi(1, 1, 2, 1)
+        loop_gain(0, 0, 5, (0, 1))
+        add_one(0, 1, 4)
+        combine_gi(1, 1, 3, 1)
+        fill(2, 0, 0, 0)
+        scale_sum(1, 1, 1, 7)
+        combine(2, 0, 0, 0)
+        square(0, 1, 4)
+        loop_gain(0, 2, 3, (0, 1))
+        interleave_h(2)
+        quantize_h(2)
+        add_one(0, 0, 5)
+        interleave_h(3)
+        fill(2, 0, 1, 1)
+        fill(2, 0, 2, 2)
+        combine(2, 0, 1, 1)
+        fill(2, 0, 3, 0)
+        fill_sum(1, 1, 3, 7)
+        scale_sum(1, 1, 2, 6)
+        loop_gain(0, 3, 6, (0, 1))
+        combine(2, 0, 2, 2)
+        fill(2, 1, 0, 1)
+        square(0, 0, 5)
+        square_diagonal(0, 0, 2)
+        scale_sum(1, 1, 3, 7)
+        combine(2, 0, 3, 0)
+        combine(2, 1, 0, 1)
+        square(0, 2, 3)
+        fill(2, 1, 1, 2)
+        interleave_h_part(4, 0, "A")
+        fill(2, 1, 2, 0)
+        sum_squares(0, 0, 2, 7, 2)
+        fill(2, 1, 3, 1)
+        add_one(0, 3, 6)
+        combine(2, 1, 1, 2)
+        fill(3, 0, 0, 2)
+        combine(2, 1, 2, 0)
+        root(0, 0, 2, 7)
+        store_root(0, 0, 2)
+        add_one(0, 2, 3)
+        square(0, 3, 6)
+        quantize_h(3)
+        fill(3, 0, 1, 0)
+        loop_gain(1, 0, 4, (0, 1))
+        loop_gain(1, 1, 3, (0, 1))
+        combine(2, 1, 3, 1)
+        interleave_h_part(4, 1, "G")
+        combine(3, 0, 0, 2)
+        add_one(1, 0, 4)
+        combine(3, 0, 1, 0)
+        quantize_h_part(4, 0, "A")
+        fill(3, 0, 2, 1)
+        loop_gain(1, 3, 7, (0, 1))
+        quantize_h_part(4, 1, "G")
+        fill(3, 0, 3, 2)
+        square_diagonal(0, 2, 2)
+        interleave_h_part(5, 1, "G")
+        interleave_h_part(5, 0, "A")
+        fill(3, 1, 0, 0)
+        add_one(1, 1, 3)
+        quantize_h_part(5, 0, "A")
+        combine(3, 0, 2, 1)
+        square(1, 0, 4)
+        square(1, 3, 7)
+        loop_gain(1, 2, 6, (0, 1))
+        square(1, 1, 3)
+        combine(3, 0, 3, 2)
+        sum_squares(0, 2, 2, 5, 2)
+        square(1, 2, 6)
+        fill(3, 1, 1, 1)
+        combine(3, 1, 0, 0)
+        add_one(1, 3, 7)
+        add_one(1, 2, 6)
+        fill(3, 1, 2, 2)
+        square_diagonal(1, 0, 2)
+        fill(3, 1, 3, 0)
+        quantize_h_part(5, 1, "G")
+        root(0, 2, 2, 5)
         store_root(0, 2, 2)
-        scale_gr(12, (1,))
-        interleave_h(4)
-        add_identity(1, 0, 7)
-        combine(11, (0,))
-        loop_gain(1, 1, 4, (0, 1))
-        combine(11, (1,))
-        add_identity(1, 1, 4)
-        loop_gain(1, 2, 5, (0, 1))
-        loop_gain(1, 3, 6, (0, 1))
-        square(1, 0, 7)
-        combine(10, (0,))
-        fill(13, 0)
-        add_identity(1, 2, 5)
-        add_identity(1, 3, 6)
-        scale_gr(12, (0,))
-        fill(14, 0)
-        fill(13, 1)
-        quantize_h(4)
-        fill(12, 1)
-        interleave_h(5)
-        square(1, 1, 4)
-        combine(12, (0,))
-        square(1, 2, 5)
-        combine(12, (1,))
-        sum_squares(1, 0, 2, 7)
-        square(1, 3, 6)
-        scale_gr(13, (0,))
-        scale_gr(13, (1,))
-        sum_squares(1, 2, 2, 4)
-        fill(15, 0)
-        combine(13, (0,))
-        combine(13, (1,))
-        scale_gr(14, (1,))
-        root(1, 0, 2, 7)
+        interleave_h_part(6, 0, "A")
+        combine(3, 1, 1, 1)
+        interleave_h_part(6, 1, "G")
+        combine(3, 1, 3, 0)
+        combine(3, 1, 2, 2)
+        square_diagonal(1, 2, 2)
+        loop_gain(2, 1, 6, (0, 1))
+        loop_gain(2, 2, 7, (0, 1))
+        square(2, 1, 6)
+        sum_squares(1, 0, 2, 5, 2)
+        interleave_h_part(7, 0, "V")
+        square(2, 2, 7)
+        root(1, 0, 2, 5)
         store_root(1, 0, 2)
-        scale_gr(14, (0,))
-        fill(14, 1)
-        scale_gr(15, (0,))
-        fill(15, 1)
-        quantize_h(5)
-        scale_gr(15, (1,))
-        interleave_h(6)
+        quantize_h_part(6, 1, "G")
+        interleave_h_part(7, 1, "V")
+        sum_squares(1, 2, 2, 4, 2)
+        quantize_h_part(6, 0, "A")
+        loop_gain(2, 0, 3, (0, 1))
+        quantize_h_part(7, 0, "V")
+        quantize_h_part(7, 1, "V")
+        add_one(2, 1, 6)
         root(1, 2, 2, 4)
         store_root(1, 2, 2)
-        combine(14, (0,))
-        loop_gain(2, 0, 5, (0, 1))
-        loop_gain(2, 1, 6, (0, 1))
-        add_identity(2, 0, 5)
-        combine(15, (0,))
-        loop_gain(2, 2, 7, (0, 1))
-        square(2, 0, 5)
-        add_identity(2, 1, 6)
-        square(2, 1, 6)
-        combine(15, (1,))
-        add_identity(2, 2, 7)
-        combine(14, (1,))
-        quantize_h(6)
-        loop_gain(2, 3, 4, (0, 1))
-        sum_squares(2, 0, 2, 5)
-        square(2, 2, 7)
-        square(2, 3, 4)
-        interleave_h_part(7, 0, "V")
-        interleave_h_part(7, 1, "V")
-        add_identity(2, 3, 4)
-        quantize_h_part(7, 0)
-        quantize_h_part(7, 1)
-        sum_squares(2, 2, 1, 6)
-        loop_gain(3, 2, 2, (0,))
-        loop_gain(3, 0, 0, (0,))
-        loop_gain(3, 1, 1, (0,))
-        loop_gain(3, 3, 4, (0,))
-        loop_gain(3, 0, 0, (1,))
-        root(2, 0, 2, 5)
-        store_root(2, 0, 2)
-        loop_gain(3, 1, 1, (1,))
-        loop_gain(3, 2, 2, (1,))
-        root(2, 2, 1, 6)
-        store_root(2, 2, 1)
-        loop_gain(3, 3, 4, (1,))
-        square(3, 0, 0)
-        round_result(0, 0, 2, "V")
-        round_result(0, 2, 2, "V")
-        add_identity(3, 1, 1)
-        add_identity(3, 0, 0)
-        sum_squares(2, 3, 1, 7)
-        add_identity(3, 2, 2)
-        square(3, 1, 1)
-        sum_squares(3, 0, 2, 3)
-        square(3, 3, 4)
-        square(3, 2, 2)
+        loop_gain(2, 3, 5, (0, 1))
+        add_one(2, 2, 7)
+        square(2, 0, 3)
+        loop_gain(3, 1, 2, (0,))
+        loop_gain(3, 2, 0, (0,))
+        add_one(2, 0, 3)
+        loop_gain(3, 2, 0, (1,))
+        square(2, 3, 5)
+        loop_gain(3, 0, 1, (0,))
+        square_diagonal(2, 2, 1)
+        square_diagonal(2, 0, 2)
+        add_one(2, 3, 5)
+        loop_gain(3, 1, 2, (1,))
+        square(3, 2, 0)
+        square(3, 1, 2)
+        loop_gain(3, 0, 1, (1,))
+        square(3, 0, 1)
+        round_result(0, 2, 2, "G")
+        add_one(3, 2, 0)
+        add_one(3, 1, 2)
+        round_result(0, 0, 2, "G")
+        square_diagonal(3, 2, 1)
+        add_one(3, 0, 1)
+        sum_squares(2, 0, 2, 4, 2)
+        loop_gain(3, 3, 7, (0,))
         quantize_result(0, 2, 2)
         store_codes(0, 2, 2)
-        add_identity(3, 3, 4)
         quantize_result(0, 0, 2)
         store_codes(0, 0, 2)
-        root(2, 3, 1, 7)
-        store_root(2, 3, 1)
-        sum_squares(3, 3, 1, 6)
-        root(3, 0, 2, 3)
-        store_root(3, 0, 2)
-        round_result(1, 0, 2, "V")
-        root(3, 3, 1, 6)
-        store_root(3, 3, 1)
-        sum_squares(3, 2, 1, 5)
-        root(3, 2, 1, 5)
+        loop_gain(3, 3, 7, (1,))
+        root(2, 0, 2, 4)
+        store_root(2, 0, 2)
+        square_diagonal(3, 0, 2)
+        square_diagonal(2, 3, 1)
+        sum_squares(2, 2, 1, 3, 2)
+        sum_squares(3, 2, 1, 4, 2)
+        sum_squares(3, 0, 2, 5, 2)
+        square(3, 3, 7)
+        add_one(3, 3, 7)
+        sum_squares(2, 3, 1, 6, 2)
+        root(2, 2, 1, 3)
+        store_root(2, 2, 1)
+        root(3, 2, 1, 4)
         store_root(3, 2, 1)
-        round_result(1, 3, 1, "V")
+        square_diagonal(3, 3, 1)
+        root(3, 0, 2, 5)
+        store_root(3, 0, 2)
         round_result(1, 2, 1, "V")
+        quantize_result(1, 2, 1)
+        store_codes(1, 2, 1)
+        sum_squares(3, 3, 1, 3, 2)
+        root(2, 3, 1, 6)
+        store_root(2, 3, 1)
+        root(3, 3, 1, 3)
+        store_root(3, 3, 1)
+        round_result(1, 0, 2, "V")
+        round_result(1, 3, 1, "V")
         quantize_result(1, 0, 2)
         store_codes(1, 0, 2)
         quantize_result(1, 3, 1)
         store_codes(1, 3, 1)
-        quantize_result(1, 2, 1)
-        store_codes(1, 2, 1)
         store_scales()

import math
from contextlib import ExitStack

import concourse.mybir as mybir
from concourse.masks import make_identity

F32 = mybir.dt.float32
BF16 = mybir.dt.bfloat16
I32 = mybir.dt.int32
U32 = mybir.dt.uint32
U8 = mybir.dt.uint8
FP8X4 = mybir.dt.float8_e4m3fn_x4
FP4X4 = mybir.dt.float4_e2m1fn_x4
ALU = mybir.AluOpType
ACT = mybir.ActivationFunctionType

W, P, R, M = 2, 512, 512, 1024
FLOPS = 2 * W * 2 * (P * R * M + P * M * P)

PARTS = 128
PACK = 4
GROUPS = M // 512
HALF = 256
UNITS = 4
STEPS = 16
CRB = [0,1,2,3,1,0,4,5]
CHUNKS = [[[0,2],[2,2]],[[0,2],[2,1],[3,1]]]


def tile_delayedmodalloopreturndifferencemagnitud_x2_kernel(
    tc, c, b_words, b_scales, k_words, k_scales, alpha, beta, omega, tau, out_0, out_1, out_2
):
    nc = tc.nc
    with ExitStack() as ctx:
        sb = ctx.enter_context(tc.tile_pool(name="sb", bufs=1))
        ps = ctx.enter_context(tc.psum_pool(name="ps", bufs=1))
        ctx.enter_context(tc.manual_schedule())

        def sbuf(name, shape, dtype):
            return sb.tile(shape, dtype, name=name, align_bytes=64)

        banks = [ps.tile([PARTS, 512], F32, name="bank%d" % i) for i in range(8)]

        alpha_sb = sbuf("alpha_sb", [PARTS, PACK], BF16)
        beta_sb = sbuf("beta_sb", [PARTS, PACK], BF16)
        omega_word = sbuf("omega_word", [PARTS, 1], F32)
        omega_sb = sbuf("omega_sb", [PARTS, W], F32)
        omega_neg = sbuf("omega_neg", [PARTS, W], F32)
        tau_sb = sbuf("tau_sb", [PARTS, GROUPS, PACK], BF16)
        c_sb = [sbuf("c_sb%d" % i, [PARTS, 2, R], BF16) for i in range(2)]
        bw_raw = sbuf("bw_raw", [PARTS, 2 * M], U8)
        bs_raw = sbuf("bs_raw", [PARTS, M], U8)
        bw = sbuf("bw", [PARTS, GROUPS, PACK, 256], U8)
        bs = sbuf("bs", [PARTS, GROUPS, PACK, PARTS], U8)
        kw = sbuf("kw", [PARTS, GROUPS, 2 * P], U8)
        ks = sbuf("ks", [PARTS, GROUPS, P], U8)
        ident = sbuf("ident", [PARTS, PARTS], F32)

        ident2 = sbuf("ident2", [PARTS, PARTS], F32)
        cross = sbuf("cross", [PARTS, 4, 2, PARTS], F32)
        warm = sbuf("warm", [PARTS, 2], F32)
        warm2 = sbuf("warm2", [PARTS, 1], F32)
        c_rows = c.rearrange("(q t) r -> q t r", t=PACK)

        def clear_first():
            nc.vector.memset(omega_word[:], 0.0)
            nc.vector.memset(bs_raw[:].bitcast(I32), 0)
            nc.vector.memset(warm[:, 0:1], 1.0)
            nc.vector.memset(ks[:].rearrange("p g n -> p (g n)").bitcast(I32), 0)

        def load_vectors():
            nc.scalar.dma_start(out=beta_sb[:], in_=beta.rearrange("(p j) -> p j", j=PACK))
            nc.scalar.dma_start(out=alpha_sb[:], in_=alpha.rearrange("(p j) -> p j", j=PACK))
            nc.scalar.dma_start(out=omega_word[0:1, :].bitcast(BF16), in_=omega.rearrange("(o w) -> o w", o=1))
            nc.scalar.activation(out=warm[:, 1:2], in_=warm[:, 0:1], func=ACT.Sin)

        def load_matrices():
            nc.sync.dma_start(out=c_sb[0][:], in_=c_rows[:, 0:2, :])
            nc.sync.dma_start(out=bw_raw[:].bitcast(I32), in_=b_words[0].bitcast(I32))
            for q in range(4):
                nc.sync.dma_start(
                    out=bs_raw[32 * q : 32 * q + 4, :].bitcast(I32), in_=b_scales[0, 4 * q : 4 * q + 4, :].bitcast(I32)
                )
            nc.sync.dma_start(out=tau_sb[:], in_=tau.rearrange("(g p j) -> p g j", g=GROUPS, j=PACK))
            nc.sync.dma_start(out=c_sb[1][:], in_=c_rows[:, 2:4, :])
            nc.sync.dma_start(out=kw[:].bitcast(I32), in_=k_words.rearrange("g p n -> p g n").bitcast(I32))
            for q in range(4):
                nc.sync.dma_start(
                    out=ks[32 * q : 32 * q + 4, :, :].bitcast(I32),
                    in_=k_scales[:, 4 * q : 4 * q + 4, :].rearrange("g r n -> r g n").bitcast(I32),
                )

        def spread_omega(b):
            nc.tensor.transpose(banks[b][:, 0:PARTS], omega_word[:, 0:1].to_broadcast([PARTS, PARTS]), ident[:])

        def copy_omega(b):
            omega_all = banks[b][:, 0:1].bitcast(BF16)
            nc.scalar.activation(out=omega_neg[:], in_=omega_all, func=ACT.Copy, scale=-1.0)
            nc.scalar.activation(out=omega_sb[:], in_=omega_all, func=ACT.Copy)

        def identity():
            make_identity(nc, ident[:])

        def clear_cross():
            nc.gpsimd.memset(cross[:], 0.0)
            nc.gpsimd.tensor_scalar(out=ident2[:], in0=ident[:], scalar1=2.0, scalar2=0.0, op0=ALU.mult, op1=ALU.add)

        def store_scales():
            for q in range(4):
                (nc.sync, nc.scalar)[q % 2].dma_start(
                    out=out_2[0, 4 * q : 4 * q + 4, :].bitcast(I32),
                    in_=out_scales[32 * q : 32 * q + 4, :].bitcast(I32),
                )

        sneg = sbuf("sneg", [PARTS, W, PACK], F32)
        a2 = sbuf("a2", [PARTS, PACK], F32)
        s2 = sbuf("s2", [PARTS, W, PACK], F32)
        den = sbuf("den", [PARTS, W, PACK], F32)
        rec = sbuf("rec", [PARTS, W, PACK], F32)
        dfac = [sbuf("dfac%d" % i, [PARTS, W, PACK], F32) for i in range(2)]
        turns = sbuf("turns", [PARTS, W, 8], F32)
        whole = sbuf("whole", [PARTS, W, 8], I32)
        f1 = sbuf("f1", [PARTS, W, 8], F32)
        f2 = sbuf("f2", [PARTS, W, 8], F32)
        frac = sbuf("frac", [PARTS, W * 8], F32)
        fabs = sbuf("fabs", [PARTS, W * 8], F32)
        co = sbuf("co", [PARTS, W * 8], F32)
        si = sbuf("si", [PARTS, W * 8], F32)
        on_gi = sbuf("on_gi", [PARTS, W * 8], F32)
        on_gr = sbuf("on_gr", [PARTS, W * 8], F32)

        def over_w(t):
            return t[:].unsqueeze(1).to_broadcast([PARTS, W, PACK])

        f1f = f1[:].rearrange("p w j -> p (w j)")
        f2f = f2[:].rearrange("p w j -> p (w j)")

        def resolvent(step):
            if step == 0:
                nc.scalar.activation(out=a2[:], in_=alpha_sb[:], func=ACT.Square)
            if step == 1:
                for w in range(W):
                    nc.scalar.activation(out=s2[:, w, :], in_=beta_sb[:], func=ACT.Square, bias=omega_neg[:, w : w + 1])
                for w in range(W):
                    nc.scalar.activation(
                        out=sneg[:, w, :], in_=beta_sb[:], func=ACT.Identity, bias=omega_neg[:, w : w + 1]
                    )
            if step == 2:
                nc.vector.tensor_tensor(out=den[:], in0=s2[:], in1=over_w(a2), op=ALU.add)
            if step == 3:
                nc.vector.reciprocal(out=rec[:], in_=den[:])
            if step == 4:
                nc.vector.tensor_tensor(out=dfac[0][:], in0=rec[:], in1=over_w(alpha_sb), op=ALU.mult)
                nc.vector.tensor_tensor(out=dfac[1][:], in0=rec[:], in1=sneg[:], op=ALU.mult)

        def phase(step):
            if step == 0:
                for w in range(W):
                    nc.vector.tensor_scalar(
                        out=turns[:, w, :],
                        in0=tau_sb[:].rearrange("p g j -> p (g j)"),
                        scalar1=omega_sb[:, w : w + 1],
                        scalar2=1.0 / (2.0 * math.pi),
                        op0=ALU.mult,
                        op1=ALU.mult,
                    )
            if step == 1:
                nc.vector.tensor_copy(out=whole[:], in_=turns[:])
            if step == 2:
                nc.vector.tensor_tensor(out=f1[:], in0=turns[:], in1=whole[:], op=ALU.subtract)
            if step == 3:
                nc.vector.scalar_tensor_tensor(out=f2f, in0=f1f, scalar=0.5, in1=f1f, op0=ALU.is_gt, op1=ALU.subtract)
            if step == 4:
                nc.vector.scalar_tensor_tensor(
                    out=frac[:], in0=f2f, scalar=0.5, in1=f2f, op0=ALU.is_gt, op1=ALU.subtract
                )
            if step == 5:
                nc.scalar.activation(out=fabs[:], in_=frac[:], func=ACT.Abs)

        def sines():
            nc.scalar.activation(out=si[:], in_=frac[:], func=ACT.Sin, scale=2.0 * math.pi)
            nc.scalar.activation(out=co[:], in_=fabs[:], func=ACT.Sin, scale=-2.0 * math.pi, bias=0.5 * math.pi)
            nc.scalar.activation(out=warm2[:], in_=warm[:, 0:1], func=ACT.Sqrt)

        def delay_factors():
            nc.vector.tensor_tensor(out=on_gi[:], in0=si[:], in1=co[:], op=ALU.subtract)
            nc.vector.scalar_tensor_tensor(
                out=on_gr[:], in0=si[:], scalar=-1.0, in1=co[:], op0=ALU.mult, op1=ALU.subtract
            )

        def permute_b_words(g):
            nc.vector.tensor_copy(
                out=bw[:, g, :, :].rearrange("p t (q e) -> p t q e", e=2),
                in_=bw_raw[:, 1024 * g : 1024 * (g + 1)].rearrange("p (q t e) -> p t q e", t=PACK, e=2),
            )

        def permute_b_scales(g):
            nc.vector.tensor_copy(
                out=bs[:, g, :, :], in_=bs_raw[:, 512 * g : 512 * (g + 1)].rearrange("p (q t) -> p t q", t=PACK)
            )

        crb = [sbuf("crb%d" % i, [PARTS, PACK * HALF], BF16) for i in range(6)]
        crq = [sbuf("crq%d" % i, [PARTS, P], U32) for i in range(2 * W)]
        crs = [sbuf("crs%d" % i, [PARTS, P], U8) for i in range(2 * W)]

        crp = [sbuf("crp%d" % i, [PARTS, PACK, HALF], BF16) for i in range(4)]

        def scale_c_planar(u, ri, b):
            bank = banks[b]
            for j in range(PACK):
                nc.scalar.activation(
                    out=crp[(2 * u + ri) % 4][:, j, :],
                    in_=bank[:].bitcast(BF16).rearrange("p (a n e) -> p a e n", a=2, e=2)[:, j // 2, j % 2, :],
                    func=ACT.Copy,
                    scale=dfac[ri][:, u // 2, j : j + 1],
                )

        def interleave_c(u, ri, eng):
            out = crb[CRB[2 * u + ri]][:].rearrange("p (n t) -> p n t", t=PACK)
            in_ = crp[(2 * u + ri) % 4][:].rearrange("p t n -> p n t")
            if eng == "G":
                nc.gpsimd.tensor_scalar(out=out, in0=in_, scalar1=1.0, scalar2=0.0, op0=ALU.mult, op1=ALU.add)
            else:
                nc.scalar.copy(
                    out=out.rearrange("p (c i) t -> p c t i", i=4), in_=in_.rearrange("p (c i) t -> p c t i", i=4)
                )

        def transpose_c(u, b):
            words = c_sb[u % 2][:].bitcast(F32)
            for tl in range(2):
                for pair in range(2):
                    col = 256 * pair + PARTS * tl
                    nc.tensor.transpose(banks[b][:, col : col + PARTS], words[:, tl, pair::2], ident[:])

        def scale_c(u, ri, b):
            nc.vector.tensor_tensor(
                out=crb[CRB[2 * u + ri]][:].rearrange("p (n a e) -> p n a e", a=2, e=2),
                in0=banks[b][:].bitcast(BF16).rearrange("p (a n e) -> p n a e", a=2, e=2),
                in1=dfac[ri][:, u // 2, :]
                .rearrange("p (a e) -> p a e", e=2)
                .unsqueeze(1)
                .to_broadcast([PARTS, HALF, 2, 2]),
                op=ALU.mult,
            )

        def quantize_c(u, ri):
            i = 2 * (u // 2) + ri
            cols = slice(HALF * (u % 2), HALF * (u % 2 + 1))
            nc.vector.quantize_mx(
                out=crq[i][:, cols].bitcast(FP8X4), scales=crs[i][:, cols], in_=crb[CRB[2 * u + ri]][:]
            )

        def plant_pass(out, g, t, i, cols, start, stop):
            nc.tensor.matmul_mx(
                out=out,
                lhsT=bw[:, g, t, :].bitcast(FP4X4),
                lhsT_scale=bs[:, g, t, :],
                rhs=crq[i][:, cols].bitcast(FP8X4),
                rhs_scale=crs[i][:, cols],
                start=start,
                stop=stop,
            )

        def fill(u, g, t, b):
            cols = slice(HALF * (u % 2), HALF * (u % 2 + 1))
            for ri in range(2):
                plant_pass(banks[b][:, HALF * ri : HALF * (ri + 1)], g, t, 2 * (u // 2) + ri, cols, True, True)

        def fill_sum(w, g, t, b):
            for ri in range(2):
                plant_pass(banks[b][:], g, t, 2 * w + ri, slice(0, P), ri == 0, ri == 1)

        def fill_sum_narrow(u, g, t, b):
            for tl in range(2):
                for k in range(2):
                    cols = slice(HALF * (u % 2) + PARTS * k, HALF * (u % 2) + PARTS * (k + 1))
                    dst = HALF * tl + PARTS * k
                    for ri in range(2):
                        plant_pass(
                            banks[b][:, dst : dst + PARTS], g, t + tl, 2 * (u // 2) + ri, cols, ri == 0, ri == 1
                        )

        shared = [sbuf("shared%d" % i, [PARTS, P], F32) for i in range(8)]
        hpl = [sbuf("hpl%d" % i, [PARTS, 2, PACK, HALF], BF16) for i in range(3)]
        hil = sbuf("hil", [PARTS, 2, HALF, PACK], BF16)
        hil2 = [sbuf("hil2_%d" % i, [PARTS, HALF, PACK], BF16) for i in range(2)]
        hq = [sbuf("hq%d" % i, [PARTS, 2 * HALF], U32) for i in range(2 * UNITS)]
        hs = [sbuf("hs%d" % i, [PARTS, 2 * HALF], U8) for i in range(2 * UNITS)]

        def factor(tile, w, g, t):
            col = 8 * w + PACK * g + t
            return tile[:, col : col + 1]

        def scale_sum(w, g, t, b):
            nc.scalar.activation(
                out=shared[PACK * g + t][:], in_=banks[b][:], func=ACT.Copy, scale=factor(co, w, g, t)
            )

        def scale_sum_narrow(u, g, t, tl, b):
            w = u // 2
            nc.scalar.activation(
                out=part[PACK * g + t + tl][:, 0, :],
                in_=banks[b][:, HALF * tl : HALF * (tl + 1)],
                func=ACT.Copy,
                scale=factor(co, w, g, t + tl),
            )

        def combine(u, g, t, b):
            w = u // 2
            for ri in range(2):
                nc.vector.scalar_tensor_tensor(
                    out=hpl[(2 * u + g) % 3][:, ri, t, :],
                    in0=banks[b][:, HALF * (1 - ri) : HALF * (2 - ri)],
                    scalar=factor((on_gi, on_gr)[ri], w, g, t),
                    in1=shared[PACK * g + t][:, HALF * (u % 2) : HALF * (u % 2 + 1)] if w else part[PACK * g + t][:, 0, :],
                    op0=ALU.mult,
                    op1=ALU.add,
                )

        part = [sbuf("part%d" % i, [PARTS, 2, HALF], F32) for i in range(8)]

        def fill_pair(u, g, j, ri, b):
            cols = slice(HALF * (u % 2), HALF * (u % 2 + 1))
            for tl in range(2):
                plant_pass(banks[b][:, HALF * tl : HALF * (tl + 1)], g, 2 * j + tl, 2 * (u // 2) + ri, cols, True, True)

        def scale_gr(u, g, t, b):
            for ri in range(2):
                nc.scalar.activation(
                    out=part[PACK * g + t][:, ri, :],
                    in_=banks[b][:, HALF * (t % 2) : HALF * (t % 2 + 1)],
                    func=ACT.Copy,
                    scale=factor((co, si)[ri], u // 2, g, t),
                )

        def combine_gi(u, g, t, b):
            for ri in range(2):
                nc.vector.scalar_tensor_tensor(
                    out=hpl[(2 * u + g) % 3][:, ri, t, :],
                    in0=banks[b][:, HALF * (t % 2) : HALF * (t % 2 + 1)],
                    scalar=factor((si, co)[ri], u // 2, g, t),
                    in1=part[PACK * g + t][:, ri, :],
                    op0=ALU.mult,
                    op1=(ALU.add, ALU.subtract)[ri],
                )

        def interleave_h(s):
            nc.gpsimd.tensor_scalar(
                out=hil[:],
                in0=hpl[s % 3][:].rearrange("p r t n -> p r n t"),
                scalar1=1.0,
                scalar2=0.0,
                op0=ALU.mult,
                op1=ALU.add,
            )

        def quantize_h(s):
            nc.vector.quantize_mx(
                out=hq[s][:].bitcast(FP8X4), scales=hs[s][:], in_=hil[:].rearrange("p r n t -> p (r n t)")
            )

        def part_buffer(s, ri, eng):
            return hil2[(s + ri) % 2][:] if eng == "A" else hil[:, ri, :, :]

        def interleave_h_part(s, ri, eng):
            out = part_buffer(s, ri, eng)
            in_ = hpl[s % 3][:, ri, :, :]
            if eng == "G":
                nc.gpsimd.tensor_scalar(
                    out=out, in0=in_.rearrange("p t n -> p n t"), scalar1=1.0, scalar2=0.0, op0=ALU.mult, op1=ALU.add
                )
            else:
                copy = nc.scalar.copy if eng == "A" else nc.vector.tensor_copy
                copy(out=out.rearrange("p (c i) t -> p c t i", i=4), in_=in_.rearrange("p t (c i) -> p c t i", i=4))

        def quantize_h_part(s, ri, eng):
            cols = slice(HALF * ri, HALF * (ri + 1))
            nc.vector.quantize_mx(
                out=hq[s][:, cols].bitcast(FP8X4),
                scales=hs[s][:, cols],
                in_=part_buffer(s, ri, eng).rearrange("p n t -> p (n t)"),
            )

        sq = [sbuf("sq%d" % i, [PARTS, 4 * 544], F32) for i in range(2)]
        res = {
            (w, j0): sbuf("res%d_%d" % (w, j0), [PARTS, PACK, PARTS * nj], F32)
            for w in range(W)
            for j0, nj in CHUNKS[w]
        }
        resb = [sbuf("resb%d" % i, [PARTS, P, PACK], BF16) for i in range(W)]
        out_codes = sbuf("out_codes", [PARTS, W * P], U32)
        out_scales = sbuf("out_scales", [PARTS, W * P], U8)

        def loop_gain(u, j, b, groups=(0, 1)):
            bank = banks[b]
            for g in groups:
                nc.tensor.matmul_mx(
                    out=bank[:],
                    lhsT=kw[:, g, 256 * j : 256 * (j + 1)].bitcast(FP4X4),
                    lhsT_scale=ks[:, g, PARTS * j : PARTS * (j + 1)],
                    rhs=hq[2 * u + g][:].bitcast(FP8X4),
                    rhs_scale=hs[2 * u + g][:],
                    start=(g == 0),
                    stop=(g == GROUPS - 1),
                )

        def square(u, j, b):
            bank = banks[b]
            nc.scalar.activation(out=sq[u % 2][:, 512 * j : 512 * (j + 1)], in_=bank[:], func=ACT.Square)

        def add_identity(u, j, b):
            t0 = 2 * (u % 2)
            nc.vector.scalar_tensor_tensor(
                out=cross[:, j, :, 32 * j : 32 * (j + 1)],
                in0=banks[b][:, 0:HALF].rearrange("p (t q) -> p t q", t=2)[:, :, 32 * j : 32 * (j + 1)],
                scalar=0.5,
                in1=ident2[:].rearrange("p (q t) -> p t q", t=PACK)[:, t0 : t0 + 2, :],
                op0=ALU.add,
                op1=ALU.mult,
            )

        diag = [sbuf("diag%d" % i, [PARTS, 4, 2, 32], F32) for i in range(2)]

        def add_one(u, j, b):
            t0 = 2 * (u % 2)
            nc.vector.tensor_tensor(
                out=diag[u % 2][:, j, :, :],
                in0=banks[b][:, 0:HALF].rearrange("p (t q) -> p t q", t=2)[:, :, 32 * j : 32 * (j + 1)],
                in1=ident[:].rearrange("p (q t) -> p t q", t=PACK)[:, t0 : t0 + 2, :],
                op=ALU.add,
            )

        def square_diagonal(u, j0, nj):
            blocks = sq[u % 2][:].rearrange("p (j s) -> p j s", s=544)[:, j0 : j0 + nj, 0:HALF]
            nc.scalar.activation(
                out=blocks.rearrange("p j (t q) -> p j t q", t=2)[:, :, :, 0:32],
                in_=diag[u % 2][:, j0 : j0 + nj, :, :],
                func=ACT.Square,
            )

        def sum_squares(u, j0, nj, b, nterms):
            for tl in range(2):
                for jl in range(nj):
                    j = j0 + jl
                    col = 512 * j + PARTS * tl
                    terms = (
                        sq[u % 2][:, col : col + PARTS],
                        sq[u % 2][:, col + HALF : col + HALF + PARTS],
                        cross[:, j, tl, :],
                    )
                    dst = PARTS * (nj * tl + jl)
                    for i, term in enumerate(terms[:nterms]):
                        nc.tensor.matmul(
                            out=banks[b][:, dst : dst + PARTS],
                            lhsT=term,
                            rhs=ident[:],
                            start=(i == 0),
                            stop=(i == nterms - 1),
                            is_transpose=True,
                        )

        def root(u, j0, nj, b):
            rows = slice(2 * (u % 2), 2 * (u % 2) + 2)
            nc.scalar.activation(
                out=res[u // 2, j0][:, rows, :],
                in_=banks[b][:, 0 : HALF * nj].rearrange("p (t n) -> p t n", t=2),
                func=ACT.Sqrt,
                bias=1e-6,
            )

        def store_root(u, j0, nj):
            rows = slice(2 * (u % 2), 2 * (u % 2) + 2)
            cols = slice(PARTS * j0, PARTS * (j0 + nj))
            nc.sync.dma_start(
                out=out_0[u // 2].rearrange("(q t) n -> q t n", t=PACK)[:, rows, cols],
                in_=res[u // 2, j0][:, rows, :],
            )

        def round_result(w, j0, nj, eng):
            out = resb[w][:, PARTS * j0 : PARTS * (j0 + nj), :]
            in_ = res[w, j0][:].rearrange("p t n -> p n t")
            if eng == "G":
                nc.gpsimd.tensor_scalar(out=out, in0=in_, scalar1=1.0, scalar2=0.0, op0=ALU.mult, op1=ALU.add)
            else:
                copy = nc.scalar.copy if eng == "A" else nc.vector.tensor_copy
                copy(out=out.rearrange("p (c i) t -> p c t i", i=4), in_=in_.rearrange("p (c i) t -> p c t i", i=4))

        def quantize_result(w, j0, nj):
            cols = slice(P * w + PARTS * j0, P * w + PARTS * (j0 + nj))
            nc.vector.quantize_mx(
                out=out_codes[:, cols].bitcast(FP8X4),
                scales=out_scales[:, cols],
                in_=resb[w][:, PARTS * j0 : PARTS * (j0 + nj), :].rearrange("p n t -> p (n t)"),
            )

        def store_codes(w, j0, nj):
            cols = slice(P * w + PARTS * j0, P * w + PARTS * (j0 + nj))
            nc.sync.dma_start(
                out=out_1[0].rearrange("p n t -> p (n t)").bitcast(I32)[:, cols], in_=out_codes[:, cols].bitcast(I32)
            )

        identity()
        clear_first()
        load_vectors()
        load_matrices()
        permute_b_words(0)
        spread_omega(6)
        copy_omega(6)
        resolvent(0)
        permute_b_scales(1)
        resolvent(1)
        phase(0)
        resolvent(2)
        phase(1)
        resolvent(3)
        phase(2)
        resolvent(4)
        transpose_c(0, 5)
        transpose_c(0, 4)
        phase(3)
        permute_b_scales(0)
        scale_c_planar(2, 0, 5)
        phase(4)
        scale_c(0, 1, 4)
        scale_c(0, 0, 4)
        permute_b_words(1)
        quantize_c(0, 0)
        transpose_c(1, 4)
        fill_pair(0, 0, 0, 0, 2)
        fill_pair(0, 0, 1, 0, 3)
        quantize_c(0, 1)
        scale_c(1, 0, 4)
        phase(5)
        scale_c_planar(2, 1, 5)
        scale_c(3, 1, 4)
        sines()
        scale_gr(0, 0, 1, 2)
        fill_pair(0, 0, 0, 1, 0)
        scale_gr(0, 0, 0, 2)
        scale_gr(0, 0, 2, 3)
        fill_pair(0, 0, 1, 1, 1)
        scale_c_planar(3, 0, 4)
        combine_gi(0, 0, 1, 0)
        combine_gi(0, 0, 0, 0)
        delay_factors()
        interleave_c(2, 1, "G")
        fill_pair(0, 1, 0, 0, 2)
        combine_gi(0, 0, 2, 1)
        scale_gr(0, 0, 3, 3)
        fill_pair(0, 1, 1, 0, 3)
        fill_pair(0, 1, 0, 1, 0)
        interleave_c(3, 0, "A")
        interleave_c(2, 0, "G")
        quantize_c(3, 1)
        combine_gi(0, 0, 3, 1)
        quantize_c(2, 1)
        fill_pair(0, 1, 1, 1, 1)
        scale_gr(0, 1, 1, 2)
        quantize_c(1, 0)
        scale_gr(0, 1, 3, 3)
        quantize_c(2, 0)
        quantize_c(3, 0)
        scale_gr(0, 1, 2, 3)
        scale_gr(0, 1, 0, 2)
        scale_c(1, 1, 4)
        fill_sum(1, 0, 0, 6)
        fill_sum(1, 0, 1, 7)
        interleave_h(0)
        scale_sum(1, 0, 0, 6)
        combine_gi(0, 1, 1, 0)
        fill_pair(1, 0, 0, 0, 2)
        fill_pair(1, 0, 1, 0, 3)
        combine_gi(0, 1, 2, 1)
        scale_sum(1, 0, 1, 7)
        scale_gr(1, 0, 0, 2)
        combine_gi(0, 1, 0, 0)
        scale_gr(1, 0, 1, 2)
        combine_gi(0, 1, 3, 1)
        fill_sum(1, 0, 2, 6)
        fill_sum(1, 0, 3, 7)
        scale_sum(1, 0, 2, 6)
        scale_gr(1, 0, 3, 3)
        scale_gr(1, 0, 2, 3)
        quantize_c(1, 1)
        quantize_h(0)
        fill_pair(1, 0, 0, 1, 0)
        fill_pair(1, 0, 1, 1, 1)
        fill_pair(1, 1, 0, 0, 2)
        combine_gi(1, 0, 1, 0)
        fill_sum(1, 1, 0, 6)
        scale_sum(1, 0, 3, 7)
        combine_gi(1, 0, 0, 0)
        fill_pair(1, 1, 1, 0, 3)
        combine_gi(1, 0, 2, 1)
        scale_sum(1, 1, 0, 6)
        combine_gi(1, 0, 3, 1)
        interleave_h(1)
        scale_gr(1, 1, 0, 2)
        fill_pair(1, 1, 0, 1, 0)
        fill_sum(1, 1, 1, 7)
        scale_gr(1, 1, 1, 2)
        quantize_h(1)
        fill_pair(1, 1, 1, 1, 1)
        fill_sum(1, 1, 2, 6)
        combine_gi(1, 1, 0, 0)
        scale_gr(1, 1, 2, 3)
        combine_gi(1, 1, 1, 0)
        scale_gr(1, 1, 3, 3)
        loop_gain(0, 1, 4, (0, 1))
        combine_gi(1, 1, 2, 1)
        loop_gain(0, 0, 5, (0, 1))
        add_one(0, 1, 4)
        combine_gi(1, 1, 3, 1)
        fill(2, 0, 0, 0)
        scale_sum(1, 1, 1, 7)
        combine(2, 0, 0, 0)
        square(0, 1, 4)
        loop_gain(0, 2, 3, (0, 1))
        interleave_h(2)
        quantize_h(2)
        add_one(0, 0, 5)
        interleave_h(3)
        fill(2, 0, 1, 1)
        fill(2, 0, 2, 2)
        combine(2, 0, 1, 1)
        fill(2, 0, 3, 0)
        fill_sum(1, 1, 3, 7)
        scale_sum(1, 1, 2, 6)
        loop_gain(0, 3, 6, (0, 1))
        combine(2, 0, 2, 2)
        fill(2, 1, 0, 1)
        square(0, 0, 5)
        square_diagonal(0, 0, 2)
        scale_sum(1, 1, 3, 7)
        combine(2, 0, 3, 0)
        combine(2, 1, 0, 1)
        square(0, 2, 3)
        fill(2, 1, 1, 2)
        interleave_h_part(4, 0, "A")
        fill(2, 1, 2, 0)
        sum_squares(0, 0, 2, 7, 2)
        fill(2, 1, 3, 1)
        add_one(0, 3, 6)
        combine(2, 1, 1, 2)
        fill(3, 0, 0, 2)
        combine(2, 1, 2, 0)
        root(0, 0, 2, 7)
        store_root(0, 0, 2)
        add_one(0, 2, 3)
        square(0, 3, 6)
        quantize_h(3)
        fill(3, 0, 1, 0)
        loop_gain(1, 0, 4, (0, 1))
        loop_gain(1, 1, 3, (0, 1))
        combine(2, 1, 3, 1)
        interleave_h_part(4, 1, "G")
        combine(3, 0, 0, 2)
        add_one(1, 0, 4)
        combine(3, 0, 1, 0)
        quantize_h_part(4, 0, "A")
        fill(3, 0, 2, 1)
        loop_gain(1, 3, 7, (0, 1))
        quantize_h_part(4, 1, "G")
        fill(3, 0, 3, 2)
        square_diagonal(0, 2, 2)
        interleave_h_part(5, 1, "G")
        interleave_h_part(5, 0, "A")
        fill(3, 1, 0, 0)
        add_one(1, 1, 3)
        quantize_h_part(5, 0, "A")
        combine(3, 0, 2, 1)
        square(1, 0, 4)
        square(1, 3, 7)
        loop_gain(1, 2, 6, (0, 1))
        square(1, 1, 3)
        combine(3, 0, 3, 2)
        sum_squares(0, 2, 2, 5, 2)
        square(1, 2, 6)
        fill(3, 1, 1, 1)
        combine(3, 1, 0, 0)
        add_one(1, 3, 7)
        add_one(1, 2, 6)
        fill(3, 1, 2, 2)
        square_diagonal(1, 0, 2)
        fill(3, 1, 3, 0)
        quantize_h_part(5, 1, "G")
        root(0, 2, 2, 5)
        store_root(0, 2, 2)
        interleave_h_part(6, 0, "A")
        combine(3, 1, 1, 1)
        interleave_h_part(6, 1, "G")
        combine(3, 1, 3, 0)
        combine(3, 1, 2, 2)
        square_diagonal(1, 2, 2)
        loop_gain(2, 1, 6, (0, 1))
        loop_gain(2, 2, 7, (0, 1))
        square(2, 1, 6)
        sum_squares(1, 0, 2, 5, 2)
        interleave_h_part(7, 0, "V")
        square(2, 2, 7)
        root(1, 0, 2, 5)
        store_root(1, 0, 2)
        quantize_h_part(6, 1, "G")
        interleave_h_part(7, 1, "V")
        sum_squares(1, 2, 2, 4, 2)
        quantize_h_part(6, 0, "A")
        loop_gain(2, 0, 3, (0, 1))
        quantize_h_part(7, 0, "V")
        quantize_h_part(7, 1, "V")
        add_one(2, 1, 6)
        root(1, 2, 2, 4)
        store_root(1, 2, 2)
        loop_gain(2, 3, 5, (0, 1))
        add_one(2, 2, 7)
        square(2, 0, 3)
        loop_gain(3, 1, 2, (0,))
        loop_gain(3, 2, 0, (0,))
        add_one(2, 0, 3)
        loop_gain(3, 2, 0, (1,))
        square(2, 3, 5)
        loop_gain(3, 0, 1, (0,))
        square_diagonal(2, 2, 1)
        square_diagonal(2, 0, 2)
        add_one(2, 3, 5)
        loop_gain(3, 1, 2, (1,))
        square(3, 2, 0)
        square(3, 1, 2)
        loop_gain(3, 0, 1, (1,))
        square(3, 0, 1)
        round_result(0, 2, 2, "G")
        add_one(3, 2, 0)
        add_one(3, 1, 2)
        round_result(0, 0, 2, "G")
        square_diagonal(3, 2, 1)
        add_one(3, 0, 1)
        sum_squares(2, 0, 2, 4, 2)
        loop_gain(3, 3, 7, (0,))
        quantize_result(0, 2, 2)
        store_codes(0, 2, 2)
        quantize_result(0, 0, 2)
        store_codes(0, 0, 2)
        loop_gain(3, 3, 7, (1,))
        root(2, 0, 2, 4)
        store_root(2, 0, 2)
        square_diagonal(3, 0, 2)
        square_diagonal(2, 3, 1)
        sum_squares(2, 2, 1, 3, 2)
        sum_squares(3, 2, 1, 4, 2)
        sum_squares(3, 0, 2, 5, 2)
        square(3, 3, 7)
        add_one(3, 3, 7)
        sum_squares(2, 3, 1, 6, 2)
        root(2, 2, 1, 3)
        store_root(2, 2, 1)
        root(3, 2, 1, 4)
        store_root(3, 2, 1)
        square_diagonal(3, 3, 1)
        root(3, 0, 2, 5)
        store_root(3, 0, 2)
        round_result(1, 2, 1, "V")
        quantize_result(1, 2, 1)
        store_codes(1, 2, 1)
        sum_squares(3, 3, 1, 3, 2)
        root(2, 3, 1, 6)
        store_root(2, 3, 1)
        root(3, 3, 1, 3)
        store_root(3, 3, 1)
        round_result(1, 0, 2, "V")
        round_result(1, 3, 1, "V")
        quantize_result(1, 0, 2)
        store_codes(1, 0, 2)
        quantize_result(1, 3, 1)
        store_codes(1, 3, 1)
        store_scales()
